import numpy as np, ml_dtypes
CORES = [3,7,11,15,131,135,139,143]
N = 8
import mx_ref
BF = ml_dtypes.bfloat16
def entries(a):
    return np.ascontiguousarray(a.T).reshape(-1)
def table(e):
    return np.ascontiguousarray(np.reshape(e, (-1, 16)).T).astype(np.int32)
def cols(t, e):
    v = np.concatenate([t.reshape(128, -1, 4), np.zeros((128, 1, 4), BF)], axis=1)
    return np.ascontiguousarray(v[:, e]).reshape(128, -1)
def f(rng, *shape):
    return mx_ref.flush((rng.standard_normal(shape, dtype=np.float32) * np.exp2(rng.integers(-2, 3, shape[:-1] + (1,)))).astype(BF))
def wide(rng, *shape, cols=0):
    v = rng.standard_normal(shape, dtype=np.float32) * np.exp2(rng.integers(-12, 13, shape)).astype(np.float32)
    if cols: v *= np.repeat(np.exp2(rng.integers(-cols, cols + 1, shape[:-2] + (1, shape[-1] // 4))) * (rng.random(shape[:-2] + (1, shape[-1] // 4)) > 0.0625), 4, axis=-1).astype(np.float32)
    return mx_ref.flush(v.astype(BF))
T, B, NB, SUM = 512, 256, 2, 1088
SIDE = np.array([0 if c < 128 else 1 for c in CORES])
CAP = np.where(SIDE[:, None] == SIDE[None, :], 224, 48)
ST = np.cumsum(CAP, axis=1) - CAP
def lists(rng, alone=False, same=False, full=False, last=False):
    it, it2, ob, bag = np.full((N, SUM), -1), np.full((N, SUM), -1), np.full((N, SUM), -1), np.full((N, SUM), -1)
    one = rng.integers(0, T, N)
    none = rng.permutation(N) if alone else np.full(N, -1)
    for r in range(N):
        has = np.zeros((N, B), bool)
        free = np.where(np.arange(N) == none[r], 0, CAP[:, r])
        if full: has[:, rng.integers(0, B)] = True
        g = np.flatnonzero(~has.any(axis=0))
        has[rng.permutation(np.repeat(np.arange(N), free - has.sum(axis=1)))[:len(g)], g] = True
        for s in range(N):
            n = CAP[s, r]; h = has[s].sum()
            k = n if full else rng.integers(h, free[s] + 1)
            has[s, rng.permutation(np.flatnonzero(~has[s]))[:k - h]] = True
            j = np.flatnonzero(has[s]); c = rng.permutation(n)[:k]
            if last: j, c = j[::-1], np.sort(c)
            else: j = rng.permutation(j)
            u = np.full(k, one[s]) if same else rng.integers(0, T, k)
            v = (u + rng.integers(1, T, k)) % T if same else rng.integers(0, T, k)
            v = np.where(rng.random(k) < (1.0 if alone else 0.25), -1, v)
            it[s, ST[s, r] + c] = u; it2[s, ST[s, r] + c] = v; ob[s, ST[s, r] + c] = j; bag[r, ST[r, s] + c] = j
    return {"it": np.stack([table(e) for e in it]), "it2": np.stack([table(e) for e in it2]), "ob": np.stack([table(e) for e in ob]), "bag": np.stack([table(e) for e in bag])}
def setup_inputs(rng):
    return {"ex": f(rng, N, 128, 4 * T), "w": f(rng, N, 128, 512 * NB), **lists(rng)}
def setup_inputs_alone(rng):
    return {**setup_inputs(rng), **lists(rng, alone=True)}
def setup_inputs_full(rng):
    return {**setup_inputs(rng), **lists(rng, full=True)}
def setup_inputs_last(rng):
    return {**setup_inputs(rng), **lists(rng, last=True)}
def setup_inputs_same(rng):
    return {**setup_inputs(rng), **lists(rng, same=True)}
def setup_inputs_spread(rng):
    d = setup_inputs(rng); d["ex"] = wide(rng, N, 128, 4 * T, cols=6); return d
def check_inputs(d):
    b = []
    it, it2, ob, bag = [np.stack([entries(d[k][r]) for r in range(N)]) for k in ("it", "it2", "ob", "bag")]
    if it.min() < -1 or it.max() >= T: b.append("it")
    if it2.min() < -1 or it2.max() >= T: b.append("it2")
    if (it2[it < 0] != -1).any(): b.append("a second item in an empty slot")
    if ob.min() < -1 or ob.max() >= B: b.append("ob")
    if bag.min() < -1 or bag.max() >= B: b.append("bag")
    for r in range(N):
        for s in range(N):
            n = CAP[s, r]; u = it[s, ST[s, r]:ST[s, r] + n]; j = bag[r, ST[r, s]:ST[r, s] + n]
            if ((u < 0) != (j < 0)).any(): b.append("bag and it differ in their empty slots")
            if (ob[s, ST[s, r]:ST[s, r] + n] != j).any(): b.append("ob and bag differ")
            j = j[j >= 0]
            if len(set(j.tolist())) != len(j): b.append("a bag named twice")
        if not set(range(B)) <= set(bag[r].tolist()): b.append("a bag without parts")
    return b
def reference(ex, w, it, it2, ob, bag):
    y = np.zeros((N, 128, B * NB), np.float32)
    for r in range(N):
        W = [mx_ref.quantize(w[r][:, 512 * o:512 * o + 512]) for o in range(NB)]
        for s in range(N):
            n = CAP[s, r]
            u, v = entries(it[s])[ST[s, r]:ST[s, r] + n], entries(it2[s])[ST[s, r]:ST[s, r] + n]
            part = (cols(ex[s], u).astype(np.float32) + cols(ex[s], v).astype(np.float32)).astype(BF)
            P = mx_ref.quantize(part)
            j = entries(bag[r])[ST[r, s]:ST[r, s] + n]; used = j >= 0
            for o in range(NB): y[r][:, B * o + j[used]] += mx_ref.matmul(W[o], P)[:, used]
    return {"y": y}

@@ -1,0 +1,361 @@
+from concourse.bass import DstId, RemoteDMATransfer
+from concourse.mybir import dt, AluOpType, ActivationFunctionType
+
+BAGS, ITEMS, ROWS = 256, 512, 16
+NEAR, FAR = 224, 48
+NC, FC = NEAR // ROWS, FAR // ROWS
+NX = 4 * FAR
+XC = 4 * FC
+LC = 4 * NC + XC
+PK = 8192
+TW = 4 * BAGS
+H = TW // 2
+EXW = 16 + 4 * ITEMS
+WINW = 592
+ACW = 416
+
+SCRATCH = {
+    "ext": ("sbuf", [128, EXW], "bfloat16"),
+    "li": ("sbuf", [128, 2 * LC], "int32"),
+    "lob": ("sbuf", [128, NC], "int32"),
+    "lbag": ("sbuf", [128, XC], "int32"),
+    "p1": ("sbuf", [128, 1], "int32"),
+    "c5": ("sbuf", [128, 1], "int32"),
+    "c4": ("sbuf", [128, 1], "int32"),
+    "c3": ("sbuf", [128, 1], "int32"),
+    "c5f": ("sbuf", [128, 1], "float32"),
+    "colf": ("sbuf", [128, 1], "float32"),
+    "tcol": ("sbuf", [128, 1], "float32"),
+    "kb": ("sbuf", [128, NC], "int32"),
+    "ksel": ("sbuf", [128, NC], "uint16"),
+    "trash": ("sbuf", [128, NC], "int32"),
+    "xtrash": ("sbuf", [128, XC], "int32"),
+    "pk1": ("sbuf", [128, 4 * NC], "float32"),
+    "pk": ("sbuf", [128, 4 * NC], "float32"),
+    "obz": ("sbuf", [128, NC], "int32"),
+    "obm": ("sbuf", [128, NC], "int32"),
+    "obo": ("sbuf", [128, NC], "uint16"),
+    "bgz": ("sbuf", [128, XC], "int32"),
+    "bgm": ("sbuf", [128, XC], "int32"),
+    "bl0": ("sbuf", [128, XC + 4], "uint16"),
+    "bl1": ("sbuf", [128, XC + 4], "uint16"),
+    "fb": ("sbuf", [128, NEAR], "float32"),
+    "ft": ("sbuf", [128, NEAR], "float32"),
+    "win": ("sbuf", [128, WINW], "int32"),
+    "offx": ("sbuf", [128, 8 * XC], "uint16"),
+    "vx": ("sbuf", [128, 4 * NX], "bfloat16"),
+    "hx": ("sbuf", [128, 4 * NX], "bfloat16"),
+    "qx": ("sbuf", [128, NX], "float8_e4m3fn_x4"),
+    "sx": ("sbuf", [128, NX], "uint8"),
+    "lqx": ("sbuf", [128, NX], "float8_e4m3fn_x4"),
+    "lsx": ("sbuf", [128, NX], "uint8"),
+    "wt": ("sbuf", [128, 1024], "bfloat16"),
+    "wq": ("sbuf", [128, 256], "float8_e4m3fn_x4"),
+    "ws": ("sbuf", [128, 256], "uint8"),
+    "xs0": ("sbuf", [128, NX], "float32"),
+    "xs1": ("sbuf", [128, NX], "float32"),
+    "acc0": ("sbuf", [128, ACW], "float32"),
+    "acc1": ("sbuf", [128, ACW], "float32"),
+    "yb": ("sbuf", [128, 2 * BAGS], "float32"),
+    "ps0": ("psum", [128, 512], "float32"),
+    "ps1": ("psum", [128, 512], "float32"),
+    "px0": ("psum", [128, 512], "float32"),
+    "px1": ("psum", [128, 512], "float32"),
+    "hd1": ("sbuf", [128, H], "bfloat16"),
+    "vd1": ("sbuf", [128, H], "bfloat16"),
+    "hd2": ("sbuf", [128, H], "bfloat16"),
+    "vd2": ("sbuf", [128, H], "bfloat16"),
+}
+for _k in "abcd":
+    SCRATCH["tab" + _k] = ("sbuf", [128, 64], "int32")
+    SCRATCH["low" + _k] = ("sbuf", [128, 64], "int32")
+    SCRATCH["ofu" + _k] = ("sbuf", [128, 64], "uint16")
+    SCRATCH["ofv" + _k] = ("sbuf", [128, 64], "uint16")
+    SCRATCH["q" + _k] = ("sbuf", [128, BAGS], "float8_e4m3fn_x4")
+    SCRATCH["s" + _k] = ("sbuf", [128, BAGS], "uint8")
+for _k in "abc":
+    SCRATCH["v" + _k] = ("sbuf", [128, TW], "bfloat16")
+    SCRATCH["h" + _k] = ("sbuf", [128, TW], "bfloat16")
+    SCRATCH["lq" + _k] = ("sbuf", [128, BAGS], "float8_e4m3fn_x4")
+    SCRATCH["ls" + _k] = ("sbuf", [128, BAGS], "uint8")
+for _c in range(4):
+    for _o in range(2):
+        SCRATCH["tm%d%d" % (_c, _o)] = ("sbuf", [128, FAR], "float32")
+
+SEMAPHORES = ["cv", "cs", "ct", "cg", "lit", "lob_s", "lbag_s", "lw", "lex", "inva", "invb", "invc", "invd",
+              "loc", "arx", "ara", "arb", "arc", "add2", "y0", "y1"]
+
+
+def rank_program(g, core, T, topo):
+    rank = T.rank_of(core)
+    if rank is None:
+        return
+    A = AluOpType
+    COPY = ActivationFunctionType.Copy
+    cores = list(T.cores)
+    near = [r for r in range(len(cores)) if topo.host(cores[r]) == topo.host(core)]
+    far = [r for r in range(len(cores)) if r not in near]
+    start, at = {}, 0
+    for r in range(len(cores)):
+        start[r] = at
+        at += NC if r in near else FC
+    m0, x0 = start[near[0]], start[far[0]]
+    mates = [r for r in near if topo.mates(core, cores[r])]
+    who = {
+        "a": [r for r in mates if topo.die(cores[r]) == topo.die(core)][0],
+        "b": [r for r in mates if topo.die(cores[r]) != topo.die(core)][0],
+        "c": [r for r in near if r != rank and cores[r] in topo.cores_of(core)][0],
+        "d": rank,
+    }
+
+    queue = {"v": g.vector, "s": g.scalar, "t": g.tensor, "g": g, "y": g.sync}
+    count = {"v": 0, "s": 0, "t": 0, "g": 0}
+    seen = {}
+
+    def done(k, ins):
+        ins.then_inc(T.sem["c" + k], 1)
+        count[k] += 1
+        return count[k]
+
+    def wait(q, name, n):
+        if seen.get((q, name), 0) < n:
+            queue[q].wait_ge(T.sem[name], n)
+            seen[(q, name)] = n
+
+    def need(q, **ks):
+        for k in ks:
+            wait(q, "c" + k, ks[k])
+
+    vec, sca, ten, syn = g.vector, g.scalar, g.tensor, g.sync
+
+    for p in range(8):
+        rows = slice(16 * p, 16 * p + 16)
+        syn.dma_start(T.li[rows, 0:LC], T.it[:, :]).then_inc(T.sem.lit, 16)
+        sca.dma_start(T.li[rows, LC:2 * LC], T.it2[:, :]).then_inc(T.sem.lit, 16)
+    for p in range(8):
+        rows = slice(16 * p, 16 * p + 16)
+        c = m0 + NC * (p // 2)
+        (syn if p % 2 == 0 else sca).dma_start(T.lob[rows, :], T.ob[:, c:c + NC]).then_inc(T.sem.lob_s, 16)
+    syn.dma_start(T.wt[:, :], T.w[:, :]).then_inc(T.sem.lw, 16)
+    for p in range(8):
+        syn.dma_start(T.lbag[16 * p:16 * p + 16, :], T.bag[:, x0:x0 + XC]).then_inc(T.sem.lbag_s, 16)
+
+    g_p = done("g", g.iota(T.p1[:, :], [[0, 1]], 0, 1))
+    g_kb = done("g", g.iota(T.kb[:, :], [[2, NC // 2], [0, 2]], 0, 0))
+    g_tr = done("g", g.iota(T.trash[:, :], [[16, NC]], BAGS, 1))
+    g.dma_start(T.ext[:, 16:EXW], T.ex[:, :]).then_inc(T.sem.lex, 16)
+    g_xt = done("g", g.iota(T.xtrash[:, :], [[0, 4], [16, FC]], BAGS, 1))
+
+    v_ext = done("v", vec.memset(T.ext[:, 0:16], 0.0))
+    v_win = done("v", vec.memset(T.win[:, 0:BAGS], 0))
+    need("v", g=g_p)
+    v5 = done("v", vec.tensor_scalar(T.c5[:, :], T.p1[:, :], 5, None, A.arith_shift_right))
+    v4 = done("v", vec.tensor_scalar(T.c4[:, :], T.p1[:, :], 4, 1, A.arith_shift_right, A.bitwise_and))
+    v3 = done("v", vec.tensor_scalar(T.c3[:, :], T.p1[:, :], 3, None, A.bitwise_and))
+    need("v", v=v5)
+    v5f = done("v", vec.tensor_scalar(T.c5f[:, :], T.c5[:, :], float(NC), None, A.mult))
+    need("v", v=v3)
+    v_tc = done("v", vec.tensor_scalar(T.tcol[:, :], T.c3[:, :], 12.0, None, A.add))
+    need("v", v=v5f)
+    v_cf = done("v", vec.tensor_tensor(T.colf[:, :], T.c5f[:, :], T.c4[:, :], A.add))
+    need("v", v=v_cf, g=g_kb)
+    v_k = done("v", vec.tensor_scalar(T.ksel[:, :], T.kb[:, :], T.colf[:, 0:1], None, A.add))
+    done("v", vec.memset(T.acc0[:, :], 0.0))
+    v_acc = done("v", vec.memset(T.acc1[:, :], 0.0))
+
+    wait("v", "lit", 256)
+    v1 = done("v", vec.tensor_scalar(T.pk1[:, :], T.li[:, LC + m0:LC + m0 + 4 * NC], float(PK), float(PK + 1),
+                                     A.mult, A.add))
+    need("v", v=v1)
+    v_pk = done("v", vec.tensor_tensor(T.pk[:, :], T.pk1[:, :], T.li[:, m0:m0 + 4 * NC], A.add))
+    need("s", v=v_pk)
+    s_fb = done("s", sca.activation(T.fb[:, :], T.pk[:, :].indirect(T.ksel[:, 0:NC]), COPY))
+
+    def offx(w, t):
+        return T.offx[:, (4 * w + t) * XC:(4 * w + t + 1) * XC]
+
+    def make_offx(w, t):
+        c = LC * w + x0
+        return done("v", vec.tensor_scalar(offx(w, t), T.li[:, c:c + XC], 4.0, float(16 + t), A.mult, A.add))
+
+    v_ox = {}
+    v_ox[1, 0] = make_offx(1, 0)
+    wait("v", "lob_s", 128)
+    vz = done("v", vec.tensor_scalar(T.obz[:, :], T.lob[:, :], 1023, None, A.bitwise_and))
+    v_ox[1, 1] = make_offx(1, 1)
+    need("v", v=vz, g=g_tr)
+    vm = done("v", vec.tensor_tensor(T.obm[:, :], T.obz[:, :], T.trash[:, :], A.min))
+    v_ox[1, 2] = make_offx(1, 2)
+    need("v", v=vm)
+    vo = done("v", vec.tensor_copy(T.obo[:, :], T.obm[:, :]))
+    v_ox[1, 3] = make_offx(1, 3)
+    need("v", s=s_fb)
+    vt = done("v", vec.transpose(T.ft[:, :], T.fb[:, :]))
+    need("v", v=vt)
+    v_inv = done("v", vec.tensor_copy(T.win[:, 0:WINW].indirect(T.obo[:, 0:NC]), T.ft[:, :]))
+    need("y", v=v_inv)
+    for k in "abcd":
+        q = 32 * near.index(who[k])
+        for t in range(4):
+            syn.dma_start(T["tab" + k][t:128:4, :], T.win[q:q + 8, 0:BAGS]).then_inc(T.sem["inv" + k], 16)
+
+    wait("s", "lex", 16)
+    s_vx = {}
+    for t in range(4):
+        need("s", v=max(v_ext, v_ox[1, t]))
+        s_vx[t] = done("s", sca.activation(T.vx[:, t:4 * NX:4], T.ext[:, :].indirect(offx(1, t)), COPY))
+    for t in range(4):
+        v_ox[0, t] = make_offx(0, t)
+    wait("v", "lex", 16)
+    for t in range(4):
+        need("v", v=v_ox[0, t], s=s_vx[t])
+        vh = done("v", vec.tensor_tensor(T.hx[:, t:4 * NX:4], T.ext[:, :].indirect(offx(0, t)),
+                                         T.vx[:, t:4 * NX:4], A.add))
+    need("v", v=vh)
+    v_qx = done("v", vec.quantize_mx(T.qx[:, :], T.sx[:, :], T.hx[:, :]))
+    wait("v", "lw", 16)
+    v_qw = done("v", vec.quantize_mx(T.wq[:, :], T.ws[:, :], T.wt[:, :]))
+    wait("v", "lbag_s", 128)
+    vz = done("v", vec.tensor_scalar(T.bgz[:, :], T.lbag[:, :], 1023, None, A.bitwise_and))
+    need("v", v=vz, g=g_xt)
+    v_bm = done("v", vec.tensor_tensor(T.bgm[:, :], T.bgz[:, :], T.xtrash[:, :], A.min))
+
+    need("g", v=v_qx)
+    me = near.index(rank)
+    for src, dst in ((T.qx, T.lqx), (T.sx, T.lsx)):
+        tr = []
+        for k in range(4):
+            d = cores[far[k]]
+            es = topo.engines(core, d)
+            n = len(es) // 4
+            rid, pid = topo.addr(d, core)
+            a, b = src[:, FAR * k:FAR * k + FAR], dst[:, FAR * me:FAR * me + FAR]
+            if src is T.qx:
+                a, b = a.bitcast(dt.uint8), b.bitcast(dt.uint8)
+            tr.append(RemoteDMATransfer(dst_ids=[DstId(rid=rid, pnc=pid)], src=a, dst=b, remote_sem=T.sem.arx,
+                                        dma_engine_mask=sum(1 << e for e in es[n * k:n * k + n])))
+        g.remote_dma_fused(tr, local_sem=T.sem.loc)
+    n_x = 2 * len(topo.engines(core, cores[far[0]])) // 4
+    local = [2 * 4 * (n_x // 2)]
+    off_chip = topo.engines(core, cores[who["a"]])
+
+    v_of = {}
+
+    def unpack(k):
+        wait("v", "inv" + k, 64)
+        need("v", v=v_tc)
+        tab, low = T["tab" + k], T["low" + k]
+        v_of[k, "v"] = done("v", vec.tensor_scalar(T["ofv" + k][:, :], tab[:, :], 4.0 / PK, T.tcol[:, 0:1],
+                                                   A.mult, A.add))
+        n = done("v", vec.tensor_scalar(low[:, :], tab[:, :], PK - 1, None, A.bitwise_and))
+        need("v", v=n)
+        v_of[k, "u"] = done("v", vec.tensor_scalar(T["ofu" + k][:, :], low[:, :], 4.0, T.tcol[:, 0:1],
+                                                   A.mult, A.add))
+
+    def pick(k, u, a, b, out):
+        need("s", v=v_of[k, u])
+        return done("s", sca.activation(out, T.ext[:, :].indirect(T["of" + u + k][:, a // 4:b // 4]), COPY))
+
+    def join(k, a, b, s, second, out):
+        need("v", s=s, v=v_of[k, "u"])
+        return done("v", vec.tensor_tensor(out, T.ext[:, :].indirect(T["ofu" + k][:, a // 4:b // 4]), second, A.add))
+
+    def quant(k, a, b, tile, n):
+        need("v", v=n)
+        return done("v", vec.quantize_mx(T["q" + k][:, a:b], T["s" + k][:, a:b], tile))
+
+    def send(k, n, es):
+        need("g", v=n)
+        d = cores[who[k]]
+        rid, pid = topo.addr(d, core)
+        m = sum(1 << e for e in es)
+        g.remote_dma(T["lq" + k][:, :].bitcast(dt.uint8), T["q" + k][:, :].bitcast(dt.uint8),
+                     T.sem["ar" + k], T.sem.loc, pid, rid, m)
+        g.remote_dma(T["ls" + k][:, :], T["s" + k][:, :], T.sem["ar" + k], T.sem.loc, pid, rid, m)
+        local[0] += 2 * len(es)
+
+    unpack("a")
+    sa1 = pick("a", "v", 0, 128, T.va[:, 0:H])
+    sa2 = pick("a", "v", 128, 256, T.va[:, H:TW])
+    unpack("b")
+    need("v", v=v_bm)
+    done("v", vec.tensor_copy(T.bl0[:, 0:XC], T.bgm[:, :]))
+    v_bl = done("v", vec.tensor_copy(T.bl1[:, 1:XC + 1], T.bgm[:, :]))
+    join("a", 0, 128, sa1, T.va[:, 0:H], T.ha[:, 0:H])
+    unpack("c")
+    n = join("a", 128, 256, sa2, T.va[:, H:TW], T.ha[:, H:TW])
+    n = quant("a", 0, 256, T.ha[:, :], n)
+    send("a", n, off_chip)
+    sb = pick("b", "v", 0, 256, T.vb[:, :])
+    n = join("b", 0, 256, sb, T.vb[:, :], T.hb[:, :])
+    n = quant("b", 0, 256, T.hb[:, :], n)
+    send("b", n, off_chip)
+    unpack("d")
+    sc = pick("c", "v", 0, 256, T.vc[:, :])
+    n = join("c", 0, 256, sc, T.vc[:, :], T.hc[:, :])
+    n = quant("c", 0, 256, T.hc[:, :], n)
+    send("c", n, [e for e in topo.engines(core, cores[who["c"]]) if e in off_chip])
+
+    def mm(out, o, q, s, first, last):
+        return done("t", ten.matmul_mx(out, T.wq[:, 128 * o:128 * o + 128], T.ws[:, 128 * o:128 * o + 128],
+                                       q[:, :], s[:, :], first, last))
+
+    need("t", v=v_qw)
+    wait("t", "arx", 4 * n_x)
+    s_x = []
+    for o in range(2):
+        n = mm(T["px%d" % o][:, 0:NX], o, T.lqx, T.lsx, True, True)
+        need("s", t=n)
+        s_x.append(done("s", sca.activation(T["xs%d" % o][:, :], T["px%d" % o][:, 0:NX], COPY)))
+    s1 = pick("d", "u", 128, 256, T.hd2[:, :])
+    s2 = pick("d", "v", 128, 256, T.vd2[:, :])
+    sd = pick("d", "v", 0, 128, T.vd1[:, :])
+    need("g", s=s2)
+    g.dma_start(T.hd2[:, :], T.vd2[:, :], accum_op=A.add).then_inc(T.sem.add2, 16)
+
+    def bags(k):
+        b = T.bl0 if k % 2 == 0 else T.bl1
+        c = FC * k + k % 2
+        return b[:, c:c + FC]
+
+    prev = [v_acc, v_acc]
+    need("v", v=v_bl)
+    for k in range(4):
+        tmp = []
+        for o in range(2):
+            acc, x = T["acc%d" % o], T["xs%d" % o][:, FAR * k:FAR * k + FAR]
+            need("v", s=s_x[o], v=prev[o])
+            if k == 0:
+                tmp.append((x, prev[o]))
+            else:
+                t = T["tm%d%d" % (k, o)][:, :]
+                tmp.append((t, done("v", vec.tensor_tensor(t, acc[:, 0:ACW].indirect(bags(k)), x, A.add))))
+        for o in range(2):
+            need("v", v=tmp[o][1])
+            prev[o] = done("v", vec.tensor_copy(T["acc%d" % o][:, 0:ACW].indirect(bags(k)), tmp[o][0]))
+
+    n = join("d", 0, 128, sd, T.vd1[:, :], T.hd1[:, :])
+    quant("d", 0, 128, T.hd1[:, :], n)
+    wait("v", "add2", 16)
+    v_d = done("v", vec.quantize_mx(T.qd[:, 128:256], T.sd[:, 128:256], T.hd2[:, :]))
+
+    for k in "abc":
+        wait("t", "ar" + k, 2 * len(off_chip))
+        for o in range(2):
+            mm(T["ps%d" % o][:, 0:BAGS], o, T["lq" + k], T["ls" + k], k == "a", False)
+    need("t", v=v_d)
+    last = [mm(T["ps%d" % o][:, 0:BAGS], o, T.qd, T.sd, False, True) for o in range(2)]
+    for o in range(2):
+        need("v", t=last[o], v=prev[o])
+        for x in range(4):
+            c = BAGS * o + 64 * x
+            n = done("v", vec.tensor_tensor(T.yb[:, c:c + 64], T["ps%d" % o][:, x:BAGS:4],
+                                            T["acc%d" % o][:, 64 * x:64 * x + 64], A.add))
+        q = "ys"[o]
+        need(q, v=n)
+        queue[q].dma_start(T.y[:, BAGS * o:BAGS * o + BAGS], T.yb[:, BAGS * o:BAGS * o + BAGS]).then_inc(
+            T.sem["y%d" % o], 16)
+    wait("g", "loc", local[0])
+    wait("y", "y0", 16)
+    wait("s", "y1", 16)
+    need("y", s=count["s"], t=count["t"], g=count["g"])

@@ -7,9 +7,11 @@ NC, FC = NEAR // ROWS, FAR // ROWS
 NX = 4 * FAR
 XC = 4 * FC
 LC = 4 * NC + XC
+OX = LC + XC
 PK = 8192
 TW = 4 * BAGS
 H = TW // 2
+HB = BAGS // 2
 EXW = 16 + 4 * ITEMS
 WINW = 592
 ACW = 416
@@ -17,7 +19,7 @@ ACW = 416
 SCRATCH = {
     "ext": ("sbuf", [128, EXW], "bfloat16"),
     "li": ("sbuf", [128, 2 * LC], "int32"),
-    "lob": ("sbuf", [128, NC], "int32"),
+    "lob": ("sbuf", [128, 16], "int32"),
     "lbag": ("sbuf", [128, XC], "int32"),
     "p1": ("sbuf", [128, 1], "int32"),
     "c5": ("sbuf", [128, 1], "int32"),
@@ -32,17 +34,23 @@ SCRATCH = {
     "xtrash": ("sbuf", [128, XC], "int32"),
     "pk1": ("sbuf", [128, 4 * NC], "float32"),
     "pk": ("sbuf", [128, 4 * NC], "float32"),
-    "obz": ("sbuf", [128, NC], "int32"),
+    "obh": ("sbuf", [128, NC], "int32"),
+    "obl": ("sbuf", [128, NC], "int32"),
     "obm": ("sbuf", [128, NC], "int32"),
+    "obq": ("sbuf", [128, NC], "int32"),
+    "obs": ("sbuf", [128, NC], "int32"),
     "obo": ("sbuf", [128, NC], "uint16"),
     "bgz": ("sbuf", [128, XC], "int32"),
     "bgm": ("sbuf", [128, XC], "int32"),
-    "bl0": ("sbuf", [128, XC + 4], "uint16"),
-    "bl1": ("sbuf", [128, XC + 4], "uint16"),
+    "bl": ("sbuf", [128, 4, 2 * FC], "uint16"),
     "fb": ("sbuf", [128, NEAR], "float32"),
     "ft": ("sbuf", [128, NEAR], "float32"),
     "win": ("sbuf", [128, WINW], "int32"),
-    "offx": ("sbuf", [128, 8 * XC], "uint16"),
+    "tab": ("sbuf", [128, 256], "int32"),
+    "low": ("sbuf", [128, 256], "int32"),
+    "ofu": ("sbuf", [128, 256], "uint16"),
+    "ofv": ("sbuf", [128, 256], "uint16"),
+    "offx": ("sbuf", [128, 4 * OX], "uint16"),
     "vx": ("sbuf", [128, 4 * NX], "bfloat16"),
     "hx": ("sbuf", [128, 4 * NX], "bfloat16"),
     "qx": ("sbuf", [128, NX], "float8_e4m3fn_x4"),
@@ -52,25 +60,18 @@ SCRATCH = {
     "wt": ("sbuf", [128, 1024], "bfloat16"),
     "wq": ("sbuf", [128, 256], "float8_e4m3fn_x4"),
     "ws": ("sbuf", [128, 256], "uint8"),
-    "xs0": ("sbuf", [128, NX], "float32"),
-    "xs1": ("sbuf", [128, NX], "float32"),
-    "acc0": ("sbuf", [128, ACW], "float32"),
-    "acc1": ("sbuf", [128, ACW], "float32"),
+    "xs": ("sbuf", [128, 4, 2 * FAR], "float32"),
+    "tm": ("sbuf", [128, 4, 2 * FAR], "float32"),
+    "acc": ("sbuf", [128, 2 * ACW], "float32"),
     "yb": ("sbuf", [128, 2 * BAGS], "float32"),
-    "ps0": ("psum", [128, 512], "float32"),
-    "ps1": ("psum", [128, 512], "float32"),
     "px0": ("psum", [128, 512], "float32"),
     "px1": ("psum", [128, 512], "float32"),
+    "hd0": ("sbuf", [128, H], "bfloat16"),
+    "vd0": ("sbuf", [128, H], "bfloat16"),
     "hd1": ("sbuf", [128, H], "bfloat16"),
     "vd1": ("sbuf", [128, H], "bfloat16"),
-    "hd2": ("sbuf", [128, H], "bfloat16"),
-    "vd2": ("sbuf", [128, H], "bfloat16"),
 }
 for _k in "abcd":
-    SCRATCH["tab" + _k] = ("sbuf", [128, 64], "int32")
-    SCRATCH["low" + _k] = ("sbuf", [128, 64], "int32")
-    SCRATCH["ofu" + _k] = ("sbuf", [128, 64], "uint16")
-    SCRATCH["ofv" + _k] = ("sbuf", [128, 64], "uint16")
     SCRATCH["q" + _k] = ("sbuf", [128, BAGS], "float8_e4m3fn_x4")
     SCRATCH["s" + _k] = ("sbuf", [128, BAGS], "uint8")
 for _k in "abc":
@@ -78,12 +79,12 @@ for _k in "abc":
     SCRATCH["h" + _k] = ("sbuf", [128, TW], "bfloat16")
     SCRATCH["lq" + _k] = ("sbuf", [128, BAGS], "float8_e4m3fn_x4")
     SCRATCH["ls" + _k] = ("sbuf", [128, BAGS], "uint8")
-for _c in range(4):
-    for _o in range(2):
-        SCRATCH["tm%d%d" % (_c, _o)] = ("sbuf", [128, FAR], "float32")
+for _o in range(2):
+    for _h in range(2):
+        SCRATCH["ps%d%d" % (_o, _h)] = ("psum", [128, 512], "float32")
 
-SEMAPHORES = ["cv", "cs", "ct", "cg", "lit", "lob_s", "lbag_s", "lw", "lex", "inva", "invb", "invc", "invd",
-              "loc", "arx", "ara", "arb", "arc", "add2", "y0", "y1"]
+SEMAPHORES = ["cv", "cs", "ct", "cg", "lit", "lob_s", "lbag_s", "lw", "lex", "inva", "invb",
+              "loc", "arx", "ara", "arb", "arc", "add0", "add1", "ys"]
 
 
 def rank_program(g, core, T, topo):
@@ -128,23 +129,29 @@ def rank_program(g, core, T, topo):
 
     vec, sca, ten, syn = g.vector, g.scalar, g.tensor, g.sync
 
+    v_lob = done("v", vec.memset(T.lob[:, :], -1))
     for p in range(8):
         rows = slice(16 * p, 16 * p + 16)
         syn.dma_start(T.li[rows, 0:LC], T.it[:, :]).then_inc(T.sem.lit, 16)
         sca.dma_start(T.li[rows, LC:2 * LC], T.it2[:, :]).then_inc(T.sem.lit, 16)
-    for p in range(8):
-        rows = slice(16 * p, 16 * p + 16)
-        c = m0 + NC * (p // 2)
-        (syn if p % 2 == 0 else sca).dma_start(T.lob[rows, :], T.ob[:, c:c + NC]).then_inc(T.sem.lob_s, 16)
-    syn.dma_start(T.wt[:, :], T.w[:, :]).then_inc(T.sem.lw, 16)
-    for p in range(8):
-        syn.dma_start(T.lbag[16 * p:16 * p + 16, :], T.bag[:, x0:x0 + XC]).then_inc(T.sem.lbag_s, 16)
+    need("y", v=v_lob)
+    need("s", v=v_lob)
+    for p in range(4):
+        c = m0 + NC * p
+        (syn if p % 2 == 0 else sca).dma_start(T.lob[32 * p:32 * p + 16, 0:NC], T.ob[:, c:c + NC]).then_inc(
+            T.sem.lob_s, 16)
+    syn.dma_start(T.ext[:, 16:EXW], T.ex[:, :]).then_inc(T.sem.lex, 16)
 
     g_p = done("g", g.iota(T.p1[:, :], [[0, 1]], 0, 1))
     g_kb = done("g", g.iota(T.kb[:, :], [[2, NC // 2], [0, 2]], 0, 0))
-    g_tr = done("g", g.iota(T.trash[:, :], [[16, NC]], BAGS, 1))
-    g.dma_start(T.ext[:, 16:EXW], T.ex[:, :]).then_inc(T.sem.lex, 16)
+    g_tr = done("g", g.iota(T.trash[:, :], [[16, NC]], BAGS // 4, 1))
     g_xt = done("g", g.iota(T.xtrash[:, :], [[0, 4], [16, FC]], BAGS, 1))
+    g_acc = done("g", g.iota(T.acc[:, :], [[0, 2 * ACW]], 0, 0, allow_small_or_imprecise_dtypes=True))
+    wait("g", "lit", 256)
+    g.dma_start(T.wt[:, :], T.w[:, :]).then_inc(T.sem.lw, 16)
+    for p in range(8):
+        (syn if p % 2 == 0 else sca).dma_start(T.lbag[16 * p:16 * p + 16, :], T.bag[:, x0:x0 + XC]).then_inc(
+            T.sem.lbag_s, 16)
 
     v_ext = done("v", vec.memset(T.ext[:, 0:16], 0.0))
     v_win = done("v", vec.memset(T.win[:, 0:BAGS], 0))
@@ -160,65 +167,62 @@ def rank_program(g, core, T, topo):
     v_cf = done("v", vec.tensor_tensor(T.colf[:, :], T.c5f[:, :], T.c4[:, :], A.add))
     need("v", v=v_cf, g=g_kb)
     v_k = done("v", vec.tensor_scalar(T.ksel[:, :], T.kb[:, :], T.colf[:, 0:1], None, A.add))
-    done("v", vec.memset(T.acc0[:, :], 0.0))
-    v_acc = done("v", vec.memset(T.acc1[:, :], 0.0))
+
+    v_ox = {}
+
+    def make_offx(t):
+        v_ox[t] = done("v", vec.tensor_scalar(T.offx[:, OX * t:OX * t + OX], T.li[:, x0:x0 + OX], 4.0, float(16 + t),
+                                              A.mult, A.add))
+
+    def offx(w, t):
+        c = OX * t + LC * w
+        return T.offx[:, c:c + XC]
 
     wait("v", "lit", 256)
     v1 = done("v", vec.tensor_scalar(T.pk1[:, :], T.li[:, LC + m0:LC + m0 + 4 * NC], float(PK), float(PK + 1),
                                      A.mult, A.add))
+    make_offx(0)
     need("v", v=v1)
     v_pk = done("v", vec.tensor_tensor(T.pk[:, :], T.pk1[:, :], T.li[:, m0:m0 + 4 * NC], A.add))
     need("s", v=v_pk)
     s_fb = done("s", sca.activation(T.fb[:, :], T.pk[:, :].indirect(T.ksel[:, 0:NC]), COPY))
 
-    def offx(w, t):
-        return T.offx[:, (4 * w + t) * XC:(4 * w + t + 1) * XC]
-
-    def make_offx(w, t):
-        c = LC * w + x0
-        return done("v", vec.tensor_scalar(offx(w, t), T.li[:, c:c + XC], 4.0, float(16 + t), A.mult, A.add))
-
-    v_ox = {}
-    v_ox[1, 0] = make_offx(1, 0)
-    wait("v", "lob_s", 128)
-    vz = done("v", vec.tensor_scalar(T.obz[:, :], T.lob[:, :], 1023, None, A.bitwise_and))
-    v_ox[1, 1] = make_offx(1, 1)
-    need("v", v=vz, g=g_tr)
-    vm = done("v", vec.tensor_tensor(T.obm[:, :], T.obz[:, :], T.trash[:, :], A.min))
-    v_ox[1, 2] = make_offx(1, 2)
-    need("v", v=vm)
-    vo = done("v", vec.tensor_copy(T.obo[:, :], T.obm[:, :]))
-    v_ox[1, 3] = make_offx(1, 3)
+    wait("v", "lob_s", 64)
+    vh = done("v", vec.tensor_scalar(T.obh[:, :], T.lob[:, 0:NC], 4095, 2, A.bitwise_and, A.logical_shift_right))
+    vl = done("v", vec.tensor_scalar(T.obl[:, :], T.lob[:, 0:NC], 3, None, A.bitwise_and))
+    make_offx(1)
+    need("v", v=vl, g=g_tr)
+    done("v", vec.tensor_tensor(T.obm[:, :], T.obh[:, :], T.trash[:, :], A.min))
+    vq = done("v", vec.tensor_scalar(T.obq[:, :], T.obl[:, :], 64.0, None, A.mult))
+    make_offx(2)
+    need("v", v=vq)
+    vs = done("v", vec.tensor_tensor(T.obs[:, :], T.obq[:, :], T.obm[:, :], A.add))
+    make_offx(3)
+    need("v", v=vs)
+    vo = done("v", vec.tensor_copy(T.obo[:, :], T.obs[:, :]))
     need("v", s=s_fb)
     vt = done("v", vec.transpose(T.ft[:, :], T.fb[:, :]))
     need("v", v=vt)
     v_inv = done("v", vec.tensor_copy(T.win[:, 0:WINW].indirect(T.obo[:, 0:NC]), T.ft[:, :]))
     need("y", v=v_inv)
-    for k in "abcd":
+    for i, k in enumerate("abcd"):
         q = 32 * near.index(who[k])
         for t in range(4):
-            syn.dma_start(T["tab" + k][t:128:4, :], T.win[q:q + 8, 0:BAGS]).then_inc(T.sem["inv" + k], 16)
+            syn.dma_start(T.tab[t:128:4, 64 * i:64 * i + 64], T.win[q:q + 8, 0:BAGS]).then_inc(
+                T.sem["inva" if k == "a" else "invb"], 16)
 
     wait("s", "lex", 16)
     s_vx = {}
     for t in range(4):
-        need("s", v=max(v_ext, v_ox[1, t]))
+        need("s", v=max(v_ext, v_ox[t]))
         s_vx[t] = done("s", sca.activation(T.vx[:, t:4 * NX:4], T.ext[:, :].indirect(offx(1, t)), COPY))
-    for t in range(4):
-        v_ox[0, t] = make_offx(0, t)
     wait("v", "lex", 16)
     for t in range(4):
-        need("v", v=v_ox[0, t], s=s_vx[t])
+        need("v", s=s_vx[t])
         vh = done("v", vec.tensor_tensor(T.hx[:, t:4 * NX:4], T.ext[:, :].indirect(offx(0, t)),
                                          T.vx[:, t:4 * NX:4], A.add))
     need("v", v=vh)
     v_qx = done("v", vec.quantize_mx(T.qx[:, :], T.sx[:, :], T.hx[:, :]))
-    wait("v", "lw", 16)
-    v_qw = done("v", vec.quantize_mx(T.wq[:, :], T.ws[:, :], T.wt[:, :]))
-    wait("v", "lbag_s", 128)
-    vz = done("v", vec.tensor_scalar(T.bgz[:, :], T.lbag[:, :], 1023, None, A.bitwise_and))
-    need("v", v=vz, g=g_xt)
-    v_bm = done("v", vec.tensor_tensor(T.bgm[:, :], T.bgz[:, :], T.xtrash[:, :], A.min))
 
     need("g", v=v_qx)
     me = near.index(rank)
@@ -241,27 +245,29 @@ def rank_program(g, core, T, topo):
 
     v_of = {}
 
-    def unpack(k):
-        wait("v", "inv" + k, 64)
-        need("v", v=v_tc)
-        tab, low = T["tab" + k], T["low" + k]
-        v_of[k, "v"] = done("v", vec.tensor_scalar(T["ofv" + k][:, :], tab[:, :], 4.0 / PK, T.tcol[:, 0:1],
-                                                   A.mult, A.add))
-        n = done("v", vec.tensor_scalar(low[:, :], tab[:, :], PK - 1, None, A.bitwise_and))
+    def unpack(ks, a, b, fill=None):
+        nv = done("v", vec.tensor_scalar(T.ofv[:, a:b], T.tab[:, a:b], 4.0 / PK, T.tcol[:, 0:1], A.mult, A.add))
+        n = done("v", vec.tensor_scalar(T.low[:, a:b], T.tab[:, a:b], PK - 1, None, A.bitwise_and))
+        if fill:
+            fill()
         need("v", v=n)
-        v_of[k, "u"] = done("v", vec.tensor_scalar(T["ofu" + k][:, :], low[:, :], 4.0, T.tcol[:, 0:1],
-                                                   A.mult, A.add))
+        nu = done("v", vec.tensor_scalar(T.ofu[:, a:b], T.low[:, a:b], 4.0, T.tcol[:, 0:1], A.mult, A.add))
+        for k in ks:
+            v_of[k, "v"], v_of[k, "u"] = nv, nu
+
+    def offs(k, u, a, b):
+        c = 64 * "abcd".index(k)
+        return T["of" + u][:, c + a // 4:c + b // 4]
 
     def pick(k, u, a, b, out):
         need("s", v=v_of[k, u])
-        return done("s", sca.activation(out, T.ext[:, :].indirect(T["of" + u + k][:, a // 4:b // 4]), COPY))
+        return done("s", sca.activation(out, T.ext[:, :].indirect(offs(k, u, a, b)), COPY))
 
     def join(k, a, b, s, second, out):
         need("v", s=s, v=v_of[k, "u"])
-        return done("v", vec.tensor_tensor(out, T.ext[:, :].indirect(T["ofu" + k][:, a // 4:b // 4]), second, A.add))
+        return done("v", vec.tensor_tensor(out, T.ext[:, :].indirect(offs(k, "u", a, b)), second, A.add))
 
-    def quant(k, a, b, tile, n):
-        need("v", v=n)
+    def quant(k, a, b, tile):
         return done("v", vec.quantize_mx(T["q" + k][:, a:b], T["s" + k][:, a:b], tile))
 
     def send(k, n, es):
@@ -274,88 +280,104 @@ def rank_program(g, core, T, topo):
         g.remote_dma(T["ls" + k][:, :], T["s" + k][:, :], T.sem["ar" + k], T.sem.loc, pid, rid, m)
         local[0] += 2 * len(es)
 
-    unpack("a")
-    sa1 = pick("a", "v", 0, 128, T.va[:, 0:H])
-    sa2 = pick("a", "v", 128, 256, T.va[:, H:TW])
-    unpack("b")
-    need("v", v=v_bm)
-    done("v", vec.tensor_copy(T.bl0[:, 0:XC], T.bgm[:, :]))
-    v_bl = done("v", vec.tensor_copy(T.bl1[:, 1:XC + 1], T.bgm[:, :]))
-    join("a", 0, 128, sa1, T.va[:, 0:H], T.ha[:, 0:H])
-    unpack("c")
-    n = join("a", 128, 256, sa2, T.va[:, H:TW], T.ha[:, H:TW])
-    n = quant("a", 0, 256, T.ha[:, :], n)
+    bg = {}
+
+    def bag_first():
+        wait("v", "lbag_s", 128)
+        bg["z"] = done("v", vec.tensor_scalar(T.bgz[:, :], T.lbag[:, :], 1023, None, A.bitwise_and))
+
+    def bag_second():
+        need("v", v=bg["z"], g=g_xt)
+        bg["m"] = done("v", vec.tensor_tensor(T.bgm[:, :], T.bgz[:, :], T.xtrash[:, :], A.min))
+
+    wait("v", "inva", 64)
+    unpack("a", 0, 64, bag_first)
+    bag_second()
+    cuts = [0, 64, 128, 256]
+    sa = [pick("a", "v", a, b, T.va[:, 4 * a:4 * b]) for a, b in zip(cuts, cuts[1:])]
+    join("a", 0, 64, sa[0], T.va[:, 0:256], T.ha[:, 0:256])
+    need("v", v=bg["m"])
+    for o in range(2):
+        v_bl = done("v", vec.tensor_scalar(T.bl[:, :, FC * o:FC * o + FC], T.bgm[:, :], float(ACW * o), None, A.add))
+    join("a", 64, 128, sa[1], T.va[:, 256:512], T.ha[:, 256:512])
+    wait("v", "invb", 192)
+    unpack("bcd", 64, 256)
+    n = join("a", 128, 256, sa[2], T.va[:, H:TW], T.ha[:, H:TW])
+    need("v", v=n)
+    n = quant("a", 0, 256, T.ha[:, :])
     send("a", n, off_chip)
+    wait("v", "lw", 16)
+    v_qw = done("v", vec.quantize_mx(T.wq[:, :], T.ws[:, :], T.wt[:, :]))
     sb = pick("b", "v", 0, 256, T.vb[:, :])
     n = join("b", 0, 256, sb, T.vb[:, :], T.hb[:, :])
-    n = quant("b", 0, 256, T.hb[:, :], n)
+    need("v", v=n)
+    n = quant("b", 0, 256, T.hb[:, :])
     send("b", n, off_chip)
-    unpack("d")
     sc = pick("c", "v", 0, 256, T.vc[:, :])
     n = join("c", 0, 256, sc, T.vc[:, :], T.hc[:, :])
-    n = quant("c", 0, 256, T.hc[:, :], n)
-    send("c", n, [e for e in topo.engines(core, cores[who["c"]]) if e in off_chip])
+    need("v", v=n)
+    n_c = quant("c", 0, 256, T.hc[:, :])
+
+    def own(h):
+        pick("d", "u", HB * h, HB * h + HB, T["hd%d" % h][:, :])
+        n = pick("d", "v", HB * h, HB * h + HB, T["vd%d" % h][:, :])
+        need("g", s=n)
+        g.dma_start(T["hd%d" % h][:, :], T["vd%d" % h][:, :], accum_op=A.add).then_inc(T.sem["add%d" % h], 16)
+
+    own(0)
+    send("c", n_c, [e for e in topo.engines(core, cores[who["c"]]) if e in off_chip])
 
     def mm(out, o, q, s, first, last):
         return done("t", ten.matmul_mx(out, T.wq[:, 128 * o:128 * o + 128], T.ws[:, 128 * o:128 * o + 128],
-                                       q[:, :], s[:, :], first, last))
+                                       q, s, first, last))
 
     need("t", v=v_qw)
     wait("t", "arx", 4 * n_x)
-    s_x = []
     for o in range(2):
-        n = mm(T["px%d" % o][:, 0:NX], o, T.lqx, T.lsx, True, True)
+        n = mm(T["px%d" % o][:, 0:NX], o, T.lqx[:, :], T.lsx[:, :], True, True)
         need("s", t=n)
-        s_x.append(done("s", sca.activation(T["xs%d" % o][:, :], T["px%d" % o][:, 0:NX], COPY)))
-    s1 = pick("d", "u", 128, 256, T.hd2[:, :])
-    s2 = pick("d", "v", 128, 256, T.vd2[:, :])
-    sd = pick("d", "v", 0, 128, T.vd1[:, :])
-    need("g", s=s2)
-    g.dma_start(T.hd2[:, :], T.vd2[:, :], accum_op=A.add).then_inc(T.sem.add2, 16)
+        s_x = done("s", sca.activation(T.xs[:, :, FAR * o:FAR * o + FAR], T["px%d" % o][:, 0:NX], COPY))
+    own(1)
 
-    def bags(k):
-        b = T.bl0 if k % 2 == 0 else T.bl1
-        c = FC * k + k % 2
-        return b[:, c:c + FC]
-
-    prev = [v_acc, v_acc]
-    need("v", v=v_bl)
+    v_d = {}
+    need("v", s=s_x, v=v_bl, g=g_acc)
     for k in range(4):
-        tmp = []
-        for o in range(2):
-            acc, x = T["acc%d" % o], T["xs%d" % o][:, FAR * k:FAR * k + FAR]
-            need("v", s=s_x[o], v=prev[o])
-            if k == 0:
-                tmp.append((x, prev[o]))
-            else:
-                t = T["tm%d%d" % (k, o)][:, :]
-                tmp.append((t, done("v", vec.tensor_tensor(t, acc[:, 0:ACW].indirect(bags(k)), x, A.add))))
-        for o in range(2):
-            need("v", v=tmp[o][1])
-            prev[o] = done("v", vec.tensor_copy(T["acc%d" % o][:, 0:ACW].indirect(bags(k)), tmp[o][0]))
+        x = T.xs[:, k, :]
+        if k:
+            need("v", v=n)
+            n = done("v", vec.tensor_tensor(T.tm[:, k, :], T.acc[:, :].indirect(T.bl[:, k, :]), x, A.add))
+            if k == 3:
+                wait("v", "add0", 16)
+                v_d[0] = quant("d", 0, HB, T.hd0[:, :])
+            need("v", v=n)
+            x = T.tm[:, k, :]
+        n = done("v", vec.tensor_copy(T.acc[:, :].indirect(T.bl[:, k, :]), x))
+    v_far = n
 
-    n = join("d", 0, 128, sd, T.vd1[:, :], T.hd1[:, :])
-    quant("d", 0, 128, T.hd1[:, :], n)
-    wait("v", "add2", 16)
-    v_d = done("v", vec.quantize_mx(T.qd[:, 128:256], T.sd[:, 128:256], T.hd2[:, :]))
+    wait("v", "add1", 16)
+    v_d[1] = quant("d", HB, BAGS, T.hd1[:, :])
 
-    for k in "abc":
-        wait("t", "ar" + k, 2 * len(off_chip))
+    last = {}
+    order = ["a0", "a1", "b0", "b1", "d0", "c0", "c1", "d1"]
+    for k, h in [(x[0], int(x[1])) for x in order]:
+        if k == "d":
+            need("t", v=v_d[h])
+            q, s = T.qd, T.sd
+        else:
+            wait("t", "ar" + k, 2 * len(off_chip))
+            q, s = T["lq" + k], T["ls" + k]
+        cols = slice(HB * h, HB * h + HB)
+        last[h] = [mm(T["ps%d%d" % (o, h)][:, 0:HB], o, q[:, cols], s[:, cols], k == "a", k == "cd"[h])
+                   for o in range(2)]
+    for h in (0, 1):
         for o in range(2):
-            mm(T["ps%d" % o][:, 0:BAGS], o, T["lq" + k], T["ls" + k], k == "a", False)
-    need("t", v=v_d)
-    last = [mm(T["ps%d" % o][:, 0:BAGS], o, T.qd, T.sd, False, True) for o in range(2)]
-    for o in range(2):
-        need("v", t=last[o], v=prev[o])
-        for x in range(4):
-            c = BAGS * o + 64 * x
-            n = done("v", vec.tensor_tensor(T.yb[:, c:c + 64], T["ps%d" % o][:, x:BAGS:4],
-                                            T["acc%d" % o][:, 64 * x:64 * x + 64], A.add))
-        q = "ys"[o]
-        need(q, v=n)
-        queue[q].dma_start(T.y[:, BAGS * o:BAGS * o + BAGS], T.yb[:, BAGS * o:BAGS * o + BAGS]).then_inc(
-            T.sem["y%d" % o], 16)
+            need("v", t=last[h][o], v=v_far)
+            c = BAGS * o + HB * h
+            n = done("v", vec.tensor_tensor(T.yb[:, c:c + HB], T["ps%d%d" % (o, h)][:, 0:HB],
+                                            T.acc[:, ACW * o + HB * h:ACW * o + HB * h + HB], A.add))
+            q = "ys"[o]
+            need(q, v=n)
+            queue[q].dma_start(T.y[:, c:c + HB], T.yb[:, c:c + HB]).then_inc(T.sem.ys, 16)
     wait("g", "loc", local[0])
-    wait("y", "y0", 16)
-    wait("s", "y1", 16)
+    wait("y", "ys", 64)
     need("y", s=count["s"], t=count["t"], g=count["g"])

@@ -1,4 +1,4 @@
-from concourse.bass import DstId, RemoteDMATransfer
+from concourse.bass import DstId, IndirectOffsetOnAxis, RemoteDMATransfer
 from concourse.mybir import dt, AluOpType, ActivationFunctionType
 
 BAGS, ITEMS, ROWS = 256, 512, 16
@@ -6,34 +6,33 @@ NEAR, FAR = 224, 48
 NC, FC = NEAR // ROWS, FAR // ROWS
 NX = 4 * FAR
 XC = 4 * FC
-LC = 4 * NC + XC
-OX = LC + XC
+HC = NC // 2
 PK = 8192
 TW = 4 * BAGS
 H = TW // 2
 HB = BAGS // 2
+PIECE = 32
+CUTS = (96, 208)
 EXW = 16 + 4 * ITEMS
 WINW = 592
 ACW = 416
 
 SCRATCH = {
     "ext": ("sbuf", [128, EXW], "bfloat16"),
-    "li": ("sbuf", [128, 2 * LC], "int32"),
+    "li": ("sbuf", [128, NC], "int32"),
+    "lx": ("sbuf", [128, 2 * XC], "int32"),
     "lob": ("sbuf", [128, 16], "int32"),
-    "lbag": ("sbuf", [128, XC], "int32"),
+    "lbag": ("sbuf", [128, 4 * NC + XC], "int32"),
+    "c15": ("sbuf", [128, 1], "int32"),
     "p1": ("sbuf", [128, 1], "int32"),
-    "c5": ("sbuf", [128, 1], "int32"),
-    "c4": ("sbuf", [128, 1], "int32"),
     "c3": ("sbuf", [128, 1], "int32"),
-    "c5f": ("sbuf", [128, 1], "float32"),
-    "colf": ("sbuf", [128, 1], "float32"),
     "tcol": ("sbuf", [128, 1], "float32"),
     "kb": ("sbuf", [128, NC], "int32"),
     "ksel": ("sbuf", [128, NC], "uint16"),
     "trash": ("sbuf", [128, NC], "int32"),
     "xtrash": ("sbuf", [128, XC], "int32"),
-    "pk1": ("sbuf", [128, 4 * NC], "float32"),
-    "pk": ("sbuf", [128, 4 * NC], "float32"),
+    "pk1": ("sbuf", [128, HC], "float32"),
+    "pk": ("sbuf", [128, HC], "float32"),
     "obh": ("sbuf", [128, NC], "int32"),
     "obl": ("sbuf", [128, NC], "int32"),
     "obm": ("sbuf", [128, NC], "int32"),
@@ -50,7 +49,7 @@ SCRATCH = {
     "low": ("sbuf", [128, 256], "int32"),
     "ofu": ("sbuf", [128, 256], "uint16"),
     "ofv": ("sbuf", [128, 256], "uint16"),
-    "offx": ("sbuf", [128, 4 * OX], "uint16"),
+    "offx": ("sbuf", [128, 8 * XC], "uint16"),
     "vx": ("sbuf", [128, 4 * NX], "bfloat16"),
     "hx": ("sbuf", [128, 4 * NX], "bfloat16"),
     "qx": ("sbuf", [128, NX], "float8_e4m3fn_x4"),
@@ -83,8 +82,8 @@ for _o in range(2):
     for _h in range(2):
         SCRATCH["ps%d%d" % (_o, _h)] = ("psum", [128, 512], "float32")
 
-SEMAPHORES = ["cv", "cs", "ct", "cg", "lit", "lob_s", "lbag_s", "lw", "lex", "inva", "invb",
-              "loc", "arx", "ara", "arb", "arc", "add0", "add1", "ys"]
+SEMAPHORES = ["cv", "cs", "ct", "cg", "lit", "lf0", "lf1", "lob_s", "lbag_s", "lw", "lex", "inva", "invb", "invc",
+              "loc", "arx", "ara", "arb", "arc", "add0", "ys"]
 
 
 def rank_program(g, core, T, topo):
@@ -130,86 +129,90 @@ def rank_program(g, core, T, topo):
     vec, sca, ten, syn = g.vector, g.scalar, g.tensor, g.sync
 
     v_lob = done("v", vec.memset(T.lob[:, :], -1))
-    for p in range(8):
-        rows = slice(16 * p, 16 * p + 16)
-        syn.dma_start(T.li[rows, 0:LC], T.it[:, :]).then_inc(T.sem.lit, 16)
-        sca.dma_start(T.li[rows, LC:2 * LC], T.it2[:, :]).then_inc(T.sem.lit, 16)
+    for q in range(4):
+        rows, cols = slice(32 * q, 32 * q + 32), slice(m0 + NC * q, m0 + NC * q + NC)
+        syn.dma_start(T.li[rows, 0:HC], T.it[:, cols]).then_inc(T.sem.lit, 16)
+        sca.dma_start(T.li[rows, HC:NC], T.it2[:, cols]).then_inc(T.sem.lit, 16)
     need("y", v=v_lob)
     need("s", v=v_lob)
-    for p in range(4):
-        c = m0 + NC * p
-        (syn if p % 2 == 0 else sca).dma_start(T.lob[32 * p:32 * p + 16, 0:NC], T.ob[:, c:c + NC]).then_inc(
-            T.sem.lob_s, 16)
+    for q in range(4):
+        cols = slice(m0 + NC * q, m0 + NC * q + NC)
+        for h in range(2):
+            queue["ys"[h]].dma_start(T.lob[32 * q:32 * q + 16, HC * h:HC * h + HC],
+                                     T.ob[8 * h:8 * h + 8, cols]).then_inc(T.sem.lob_s, 16)
+    for p in range(8):
+        queue["ys"[p % 2]].dma_start(T.lx[16 * p:16 * p + 16, XC:2 * XC], T.it2[:, x0:x0 + XC]).then_inc(T.sem.lf1, 16)
     syn.dma_start(T.ext[:, 16:EXW], T.ex[:, :]).then_inc(T.sem.lex, 16)
+    for p in range(8):
+        queue["ys"[p % 2]].dma_start(T.lx[16 * p:16 * p + 16, 0:XC], T.it[:, x0:x0 + XC]).then_inc(T.sem.lf0, 16)
 
     g_p = done("g", g.iota(T.p1[:, :], [[0, 1]], 0, 1))
-    g_kb = done("g", g.iota(T.kb[:, :], [[2, NC // 2], [0, 2]], 0, 0))
+    g_kb = done("g", g.iota(T.kb[:, :], [[1, HC], [0, 2]], 0, 0))
     g_tr = done("g", g.iota(T.trash[:, :], [[16, NC]], BAGS // 4, 1))
     g_xt = done("g", g.iota(T.xtrash[:, :], [[0, 4], [16, FC]], BAGS, 1))
-    g_acc = done("g", g.iota(T.acc[:, :], [[0, 2 * ACW]], 0, 0, allow_small_or_imprecise_dtypes=True))
-    wait("g", "lit", 256)
-    g.dma_start(T.wt[:, :], T.w[:, :]).then_inc(T.sem.lw, 16)
-    for p in range(8):
-        (syn if p % 2 == 0 else sca).dma_start(T.lbag[16 * p:16 * p + 16, :], T.bag[:, x0:x0 + XC]).then_inc(
-            T.sem.lbag_s, 16)
 
     v_ext = done("v", vec.memset(T.ext[:, 0:16], 0.0))
-    v_win = done("v", vec.memset(T.win[:, 0:BAGS], 0))
     need("v", g=g_p)
-    v5 = done("v", vec.tensor_scalar(T.c5[:, :], T.p1[:, :], 5, None, A.arith_shift_right))
-    v4 = done("v", vec.tensor_scalar(T.c4[:, :], T.p1[:, :], 4, 1, A.arith_shift_right, A.bitwise_and))
+    need("g", v=done("v", vec.tensor_scalar(T.c15[:, :], T.p1[:, :], ROWS - 1, None, A.bitwise_and)))
+    g.indirect_dma_start(T.lbag[:, :], None, T.bag[:], IndirectOffsetOnAxis(ap=T.c15[:, 0:1], axis=0),
+                         bounds_check=ROWS - 1).then_inc(T.sem.lbag_s, 16)
+    wait("g", "lit", 128)
+    g.dma_start(T.wt[:, :], T.w[:, :]).then_inc(T.sem.lw, 16)
+    v_win = done("v", vec.memset(T.win[:, 0:BAGS], 0))
     v3 = done("v", vec.tensor_scalar(T.c3[:, :], T.p1[:, :], 3, None, A.bitwise_and))
-    need("v", v=v5)
-    v5f = done("v", vec.tensor_scalar(T.c5f[:, :], T.c5[:, :], float(NC), None, A.mult))
+    need("v", g=g_kb)
+    v_k = done("v", vec.tensor_copy(T.ksel[:, :], T.kb[:, :]))
     need("v", v=v3)
     v_tc = done("v", vec.tensor_scalar(T.tcol[:, :], T.c3[:, :], 12.0, None, A.add))
-    need("v", v=v5f)
-    v_cf = done("v", vec.tensor_tensor(T.colf[:, :], T.c5f[:, :], T.c4[:, :], A.add))
-    need("v", v=v_cf, g=g_kb)
-    v_k = done("v", vec.tensor_scalar(T.ksel[:, :], T.kb[:, :], T.colf[:, 0:1], None, A.add))
+    done("v", vec.memset(T.acc[:, 0:ACW], 0.0))
 
-    v_ox = {}
-
-    def make_offx(t):
-        v_ox[t] = done("v", vec.tensor_scalar(T.offx[:, OX * t:OX * t + OX], T.li[:, x0:x0 + OX], 4.0, float(16 + t),
-                                              A.mult, A.add))
-
-    def offx(w, t):
-        c = OX * t + LC * w
-        return T.offx[:, c:c + XC]
-
-    wait("v", "lit", 256)
-    v1 = done("v", vec.tensor_scalar(T.pk1[:, :], T.li[:, LC + m0:LC + m0 + 4 * NC], float(PK), float(PK + 1),
-                                     A.mult, A.add))
-    make_offx(0)
+    wait("v", "lit", 128)
+    v1 = done("v", vec.tensor_scalar(T.pk1[:, :], T.li[:, HC:NC], float(PK), float(PK + 1), A.mult, A.add))
+    done("v", vec.memset(T.acc[:, ACW:3 * ACW // 2], 0.0))
     need("v", v=v1)
-    v_pk = done("v", vec.tensor_tensor(T.pk[:, :], T.pk1[:, :], T.li[:, m0:m0 + 4 * NC], A.add))
+    v_pk = done("v", vec.tensor_tensor(T.pk[:, :], T.pk1[:, :], T.li[:, 0:HC], A.add))
     need("s", v=v_pk)
     s_fb = done("s", sca.activation(T.fb[:, :], T.pk[:, :].indirect(T.ksel[:, 0:NC]), COPY))
-
-    wait("v", "lob_s", 64)
-    vh = done("v", vec.tensor_scalar(T.obh[:, :], T.lob[:, 0:NC], 4095, 2, A.bitwise_and, A.logical_shift_right))
+    wait("v", "lob_s", 128)
     vl = done("v", vec.tensor_scalar(T.obl[:, :], T.lob[:, 0:NC], 3, None, A.bitwise_and))
-    make_offx(1)
-    need("v", v=vl, g=g_tr)
-    done("v", vec.tensor_tensor(T.obm[:, :], T.obh[:, :], T.trash[:, :], A.min))
-    vq = done("v", vec.tensor_scalar(T.obq[:, :], T.obl[:, :], 64.0, None, A.mult))
-    make_offx(2)
-    need("v", v=vq)
+    vh = done("v", vec.tensor_scalar(T.obh[:, :], T.lob[:, 0:NC], 4095, 2, A.bitwise_and, A.logical_shift_right))
+    need("v", v=vl)
+    done("v", vec.tensor_scalar(T.obq[:, :], T.obl[:, :], 64.0, None, A.mult))
+    need("v", v=vh, g=g_tr)
+    vm = done("v", vec.tensor_tensor(T.obm[:, :], T.obh[:, :], T.trash[:, :], A.min))
+    done("v", vec.memset(T.acc[:, 3 * ACW // 2:2 * ACW], 0.0))
+    need("v", v=vm)
     vs = done("v", vec.tensor_tensor(T.obs[:, :], T.obq[:, :], T.obm[:, :], A.add))
-    make_offx(3)
-    need("v", v=vs)
-    vo = done("v", vec.tensor_copy(T.obo[:, :], T.obs[:, :]))
     need("v", s=s_fb)
-    vt = done("v", vec.transpose(T.ft[:, :], T.fb[:, :]))
-    need("v", v=vt)
+    done("v", vec.transpose(T.ft[:, :], T.fb[:, :]))
+    need("v", v=vs)
+    for h in range(2):
+        vo = done("v", vec.tensor_copy(T.obo[:, h:NC:2], T.obs[:, HC * h:HC * h + HC]))
+
+    def offx(w, t):
+        c = XC * (2 * t + w)
+        return T.offx[:, c:c + XC]
+
+    def far_offsets(t, a, b):
+        c = 2 * XC * t
+        return done("v", vec.tensor_scalar(T.offx[:, c + a:c + b], T.lx[:, a:b], 4.0, float(16 + t), A.mult, A.add))
+
+    wait("v", "lf1", 128)
+    v_ox = [far_offsets(t, XC, 2 * XC) for t in (0, 1)]
+    need("v", v=vo)
     v_inv = done("v", vec.tensor_copy(T.win[:, 0:WINW].indirect(T.obo[:, 0:NC]), T.ft[:, :]))
+    wait("v", "lf0", 128)
+    v_ox += [far_offsets(t, 0, 2 * XC) for t in (2, 3)]
+    v_ou = [far_offsets(t, 0, XC) for t in (0, 1)] + v_ox[2:]
     need("y", v=v_inv)
-    for i, k in enumerate("abcd"):
-        q = 32 * near.index(who[k])
-        for t in range(4):
-            syn.dma_start(T.tab[t:128:4, 64 * i:64 * i + 64], T.win[q:q + 8, 0:BAGS]).then_inc(
-                T.sem["inva" if k == "a" else "invb"], 16)
+    def spread(eng, ts):
+        for i, k in enumerate("abcd"):
+            q = 32 * near.index(who[k])
+            for t in ts:
+                eng.dma_start(T.tab[t:128:4, 64 * i:64 * i + 64], T.win[q:q + 8, 0:BAGS]).then_inc(
+                    T.sem["inv" + min(k, "c")], 16)
+
+    spread(syn, range(4))
 
     wait("s", "lex", 16)
     s_vx = {}
@@ -218,42 +221,43 @@ def rank_program(g, core, T, topo):
         s_vx[t] = done("s", sca.activation(T.vx[:, t:4 * NX:4], T.ext[:, :].indirect(offx(1, t)), COPY))
     wait("v", "lex", 16)
     for t in range(4):
-        need("v", s=s_vx[t])
+        need("v", s=s_vx[t], v=v_ou[t])
         vh = done("v", vec.tensor_tensor(T.hx[:, t:4 * NX:4], T.ext[:, :].indirect(offx(0, t)),
                                          T.vx[:, t:4 * NX:4], A.add))
-    need("v", v=vh)
-    v_qx = done("v", vec.quantize_mx(T.qx[:, :], T.sx[:, :], T.hx[:, :]))
+    def second(a, b):
+        return done("v", vec.tensor_scalar(T.ofv[:, a:b], T.tab[:, a:b], 4.0 / PK, T.tcol[:, 0:1], A.mult, A.add))
 
-    need("g", v=v_qx)
+    def lower(a, b):
+        return done("v", vec.tensor_scalar(T.low[:, a:b], T.tab[:, a:b], PK - 1, None, A.bitwise_and))
+
+    def first(a, b, n=None):
+        if n:
+            need("v", v=n)
+        return done("v", vec.tensor_scalar(T.ofu[:, a:b], T.low[:, a:b], 4.0, T.tcol[:, 0:1], A.mult, A.add))
+
+    wait("v", "inva", 64)
+    v_of = {("a", "v"): second(0, 64)}
+    wait("v", "lbag_s", 16)
+    v_bz = done("v", vec.tensor_scalar(T.bgz[:, :], T.lbag[:, x0:x0 + XC], 1023, None, A.bitwise_and))
+    need("v", v=vh)
+    need("g", v=done("v", vec.quantize_mx(T.qx[:, :], T.sx[:, :], T.hx[:, :])))
+
     me = near.index(rank)
+    off_chip = topo.engines(core, cores[who["a"]])
+    n_x = len(off_chip) // 4
+    local = [8 * n_x]
     for src, dst in ((T.qx, T.lqx), (T.sx, T.lsx)):
         tr = []
         for k in range(4):
             d = cores[far[k]]
-            es = topo.engines(core, d)
-            n = len(es) // 4
+            es = topo.engines(core, d)[n_x * k:n_x * (k + 1)]
             rid, pid = topo.addr(d, core)
             a, b = src[:, FAR * k:FAR * k + FAR], dst[:, FAR * me:FAR * me + FAR]
             if src is T.qx:
                 a, b = a.bitcast(dt.uint8), b.bitcast(dt.uint8)
             tr.append(RemoteDMATransfer(dst_ids=[DstId(rid=rid, pnc=pid)], src=a, dst=b, remote_sem=T.sem.arx,
-                                        dma_engine_mask=sum(1 << e for e in es[n * k:n * k + n])))
+                                        dma_engine_mask=sum(1 << e for e in es)))
         g.remote_dma_fused(tr, local_sem=T.sem.loc)
-    n_x = 2 * len(topo.engines(core, cores[far[0]])) // 4
-    local = [2 * 4 * (n_x // 2)]
-    off_chip = topo.engines(core, cores[who["a"]])
-
-    v_of = {}
-
-    def unpack(ks, a, b, fill=None):
-        nv = done("v", vec.tensor_scalar(T.ofv[:, a:b], T.tab[:, a:b], 4.0 / PK, T.tcol[:, 0:1], A.mult, A.add))
-        n = done("v", vec.tensor_scalar(T.low[:, a:b], T.tab[:, a:b], PK - 1, None, A.bitwise_and))
-        if fill:
-            fill()
-        need("v", v=n)
-        nu = done("v", vec.tensor_scalar(T.ofu[:, a:b], T.low[:, a:b], 4.0, T.tcol[:, 0:1], A.mult, A.add))
-        for k in ks:
-            v_of[k, "v"], v_of[k, "u"] = nv, nu
 
     def offs(k, u, a, b):
         c = 64 * "abcd".index(k)
@@ -280,51 +284,55 @@ def rank_program(g, core, T, topo):
         g.remote_dma(T["ls" + k][:, :], T["s" + k][:, :], T.sem["ar" + k], T.sem.loc, pid, rid, m)
         local[0] += 2 * len(es)
 
-    bg = {}
-
-    def bag_first():
-        wait("v", "lbag_s", 128)
-        bg["z"] = done("v", vec.tensor_scalar(T.bgz[:, :], T.lbag[:, :], 1023, None, A.bitwise_and))
-
-    def bag_second():
-        need("v", v=bg["z"], g=g_xt)
-        bg["m"] = done("v", vec.tensor_tensor(T.bgm[:, :], T.bgz[:, :], T.xtrash[:, :], A.min))
-
-    wait("v", "inva", 64)
-    unpack("a", 0, 64, bag_first)
-    bag_second()
-    cuts = [0, 64, 128, 256]
-    sa = [pick("a", "v", a, b, T.va[:, 4 * a:4 * b]) for a, b in zip(cuts, cuts[1:])]
-    join("a", 0, 64, sa[0], T.va[:, 0:256], T.ha[:, 0:256])
-    need("v", v=bg["m"])
+    low_a = lower(0, 64)
+    need("v", v=v_bz, g=g_xt)
+    v_bm = done("v", vec.tensor_tensor(T.bgm[:, :], T.bgz[:, :], T.xtrash[:, :], A.min))
+    wait("v", "invb", 64)
+    v_of["b", "v"] = second(64, 128)
+    low_b = lower(64, 128)
+    v_of["a", "u"] = first(0, 64, low_a)
+    need("v", v=v_bm)
     for o in range(2):
         v_bl = done("v", vec.tensor_scalar(T.bl[:, :, FC * o:FC * o + FC], T.bgm[:, :], float(ACW * o), None, A.add))
-    join("a", 64, 128, sa[1], T.va[:, 256:512], T.ha[:, 256:512])
-    wait("v", "invb", 192)
-    unpack("bcd", 64, 256)
-    n = join("a", 128, 256, sa[2], T.va[:, H:TW], T.ha[:, H:TW])
+    c1, c2 = CUTS
+    sa = [pick("a", "v", a, b, T.va[:, 4 * a:4 * b]) for a, b in ((0, c1), (c1, c2))]
+    vp = done("v", vec.tensor_copy(T.va[:, 4 * c2:TW], T.ext[:, :].indirect(offs("a", "v", c2, BAGS))))
+    join("a", 0, c1, sa[0], T.va[:, 0:4 * c1], T.ha[:, 0:4 * c1])
+    v_of["b", "u"] = first(64, 128, low_b)
+    need("v", v=vp)
+    join("a", c2, BAGS, sa[0], T.va[:, 4 * c2:TW], T.ha[:, 4 * c2:TW])
+    n = join("a", c1, c2, sa[1], T.va[:, 4 * c1:4 * c2], T.ha[:, 4 * c1:4 * c2])
+    wait("v", "invc", 128)
+    v_of["c", "v"] = v_of["d", "v"] = second(128, 256)
+    v_low = lower(128, 256)
     need("v", v=n)
     n = quant("a", 0, 256, T.ha[:, :])
     send("a", n, off_chip)
-    wait("v", "lw", 16)
-    v_qw = done("v", vec.quantize_mx(T.wq[:, :], T.ws[:, :], T.wt[:, :]))
+    v_of["c", "u"] = v_of["d", "u"] = first(128, 256, v_low)
     sb = pick("b", "v", 0, 256, T.vb[:, :])
     n = join("b", 0, 256, sb, T.vb[:, :], T.hb[:, :])
+    wait("v", "lw", 16)
+    v_qw = done("v", vec.quantize_mx(T.wq[:, :], T.ws[:, :], T.wt[:, :]))
     need("v", v=n)
     n = quant("b", 0, 256, T.hb[:, :])
     send("b", n, off_chip)
     sc = pick("c", "v", 0, 256, T.vc[:, :])
     n = join("c", 0, 256, sc, T.vc[:, :], T.hc[:, :])
+
+    def upper(a, b):
+        return slice(4 * (a - HB), 4 * (b - HB))
+
+    def piece(i):
+        a, b = HB + PIECE * i, HB + PIECE * (i + 1)
+        return join("d", a, b, sd[min(i, 1)], T.vd1[:, upper(a, b)], T.hd1[:, upper(a, b)])
+
+    pick("d", "u", 0, HB, T.hd0[:, :])
+    need("g", s=pick("d", "v", 0, HB, T.vd0[:, :]))
+    g.dma_start(T.hd0[:, :], T.vd0[:, :], accum_op=A.add).then_inc(T.sem.add0, 16)
+    sd = [pick("d", "v", HB, HB + PIECE, T.vd1[:, upper(HB, HB + PIECE)])]
+    piece(0)
     need("v", v=n)
     n_c = quant("c", 0, 256, T.hc[:, :])
-
-    def own(h):
-        pick("d", "u", HB * h, HB * h + HB, T["hd%d" % h][:, :])
-        n = pick("d", "v", HB * h, HB * h + HB, T["vd%d" % h][:, :])
-        need("g", s=n)
-        g.dma_start(T["hd%d" % h][:, :], T["vd%d" % h][:, :], accum_op=A.add).then_inc(T.sem["add%d" % h], 16)
-
-    own(0)
     send("c", n_c, [e for e in topo.engines(core, cores[who["c"]]) if e in off_chip])
 
     def mm(out, o, q, s, first, last):
@@ -332,33 +340,38 @@ def rank_program(g, core, T, topo):
                                        q, s, first, last))
 
     need("t", v=v_qw)
-    wait("t", "arx", 4 * n_x)
+    wait("t", "arx", 8 * n_x)
     for o in range(2):
         n = mm(T["px%d" % o][:, 0:NX], o, T.lqx[:, :], T.lsx[:, :], True, True)
         need("s", t=n)
         s_x = done("s", sca.activation(T.xs[:, :, FAR * o:FAR * o + FAR], T["px%d" % o][:, 0:NX], COPY))
-    own(1)
+    sd.append(pick("d", "v", HB + PIECE, BAGS, T.vd1[:, upper(HB + PIECE, BAGS)]))
 
     v_d = {}
-    need("v", s=s_x, v=v_bl, g=g_acc)
-    for k in range(4):
-        x = T.xs[:, k, :]
-        if k:
-            need("v", v=n)
-            n = done("v", vec.tensor_tensor(T.tm[:, k, :], T.acc[:, :].indirect(T.bl[:, k, :]), x, A.add))
-            if k == 3:
-                wait("v", "add0", 16)
-                v_d[0] = quant("d", 0, HB, T.hd0[:, :])
-            need("v", v=n)
-            x = T.tm[:, k, :]
-        n = done("v", vec.tensor_copy(T.acc[:, :].indirect(T.bl[:, k, :]), x))
+
+    def quant_upper():
+        v_d[1] = quant("d", HB, BAGS, T.hd1[:, :])
+
+    def quant_lower():
+        wait("v", "add0", 16)
+        v_d[0] = quant("d", 0, HB, T.hd0[:, :])
+
+    fill = [lambda: piece(1), lambda: piece(2), lambda: piece(3), None, quant_upper, quant_lower, None]
+    need("v", s=s_x, v=v_bl)
+    for step in range(7):
+        k = (step + 1) // 2
+        acc = T.acc[:, :].indirect(T.bl[:, k, :])
+        if step % 2:
+            n = done("v", vec.tensor_tensor(T.tm[:, k, :], acc, T.xs[:, k, :], A.add))
+        else:
+            n = done("v", vec.tensor_copy(acc, (T.tm if k else T.xs)[:, k, :]))
+        if fill[step]:
+            fill[step]()
+        need("v", v=n)
     v_far = n
 
-    wait("v", "add1", 16)
-    v_d[1] = quant("d", HB, BAGS, T.hd1[:, :])
-
     last = {}
-    order = ["a0", "a1", "b0", "b1", "d0", "c0", "c1", "d1"]
+    order = ["a0", "a1", "b0", "b1", "d1", "c1", "c0", "d0"]
     for k, h in [(x[0], int(x[1])) for x in order]:
         if k == "d":
             need("t", v=v_d[h])
@@ -367,9 +380,9 @@ def rank_program(g, core, T, topo):
             wait("t", "ar" + k, 2 * len(off_chip))
             q, s = T["lq" + k], T["ls" + k]
         cols = slice(HB * h, HB * h + HB)
-        last[h] = [mm(T["ps%d%d" % (o, h)][:, 0:HB], o, q[:, cols], s[:, cols], k == "a", k == "cd"[h])
+        last[h] = [mm(T["ps%d%d" % (o, h)][:, 0:HB], o, q[:, cols], s[:, cols], k == "a", k == "dc"[h])
                    for o in range(2)]
-    for h in (0, 1):
+    for h in (1, 0):
         for o in range(2):
             need("v", t=last[h][o], v=v_far)
             c = BAGS * o + HB * h

from concourse.bass import DstId, IndirectOffsetOnAxis, RemoteDMATransfer
from concourse.mybir import dt, AluOpType, ActivationFunctionType

BAGS, ITEMS, ROWS = 256, 512, 16
NEAR, FAR = 224, 48
NC, FC = NEAR // ROWS, FAR // ROWS
NX = 4 * FAR
XC = 4 * FC
HC = NC // 2
PK = 8192
TW = 4 * BAGS
H = TW // 2
HB = BAGS // 2
PIECE = 32
CUTS = (96, 208)
EXW = 16 + 4 * ITEMS
WINW = 592
ACW = 416

SCRATCH = {
    "ext": ("sbuf", [128, EXW], "bfloat16"),
    "li": ("sbuf", [128, NC], "int32"),
    "lx": ("sbuf", [128, 2 * XC], "int32"),
    "lob": ("sbuf", [128, 16], "int32"),
    "lbag": ("sbuf", [128, 4 * NC + XC], "int32"),
    "c15": ("sbuf", [128, 1], "int32"),
    "p1": ("sbuf", [128, 1], "int32"),
    "c3": ("sbuf", [128, 1], "int32"),
    "tcol": ("sbuf", [128, 1], "float32"),
    "kb": ("sbuf", [128, NC], "int32"),
    "ksel": ("sbuf", [128, NC], "uint16"),
    "trash": ("sbuf", [128, NC], "int32"),
    "xtrash": ("sbuf", [128, XC], "int32"),
    "pk1": ("sbuf", [128, HC], "float32"),
    "pk": ("sbuf", [128, HC], "float32"),
    "obh": ("sbuf", [128, NC], "int32"),
    "obl": ("sbuf", [128, NC], "int32"),
    "obm": ("sbuf", [128, NC], "int32"),
    "obq": ("sbuf", [128, NC], "int32"),
    "obs": ("sbuf", [128, NC], "int32"),
    "obo": ("sbuf", [128, NC], "uint16"),
    "bgz": ("sbuf", [128, XC], "int32"),
    "bgm": ("sbuf", [128, XC], "int32"),
    "bl": ("sbuf", [128, 4, 2 * FC], "uint16"),
    "fb": ("sbuf", [128, NEAR], "float32"),
    "ft": ("sbuf", [128, NEAR], "float32"),
    "win": ("sbuf", [128, WINW], "int32"),
    "tab": ("sbuf", [128, 256], "int32"),
    "low": ("sbuf", [128, 256], "int32"),
    "ofu": ("sbuf", [128, 256], "uint16"),
    "ofv": ("sbuf", [128, 256], "uint16"),
    "offx": ("sbuf", [128, 8 * XC], "uint16"),
    "vx": ("sbuf", [128, 4 * NX], "bfloat16"),
    "hx": ("sbuf", [128, 4 * NX], "bfloat16"),
    "qx": ("sbuf", [128, NX], "float8_e4m3fn_x4"),
    "sx": ("sbuf", [128, NX], "uint8"),
    "lqx": ("sbuf", [128, NX], "float8_e4m3fn_x4"),
    "lsx": ("sbuf", [128, NX], "uint8"),
    "wt": ("sbuf", [128, 1024], "bfloat16"),
    "wq": ("sbuf", [128, 256], "float8_e4m3fn_x4"),
    "ws": ("sbuf", [128, 256], "uint8"),
    "xs": ("sbuf", [128, 4, 2 * FAR], "float32"),
    "tm": ("sbuf", [128, 4, 2 * FAR], "float32"),
    "acc": ("sbuf", [128, 2 * ACW], "float32"),
    "yb": ("sbuf", [128, 2 * BAGS], "float32"),
    "px0": ("psum", [128, 512], "float32"),
    "px1": ("psum", [128, 512], "float32"),
    "hd0": ("sbuf", [128, H], "bfloat16"),
    "vd0": ("sbuf", [128, H], "bfloat16"),
    "hd1": ("sbuf", [128, H], "bfloat16"),
    "vd1": ("sbuf", [128, H], "bfloat16"),
}
for _k in "abcd":
    SCRATCH["q" + _k] = ("sbuf", [128, BAGS], "float8_e4m3fn_x4")
    SCRATCH["s" + _k] = ("sbuf", [128, BAGS], "uint8")
for _k in "abc":
    SCRATCH["v" + _k] = ("sbuf", [128, TW], "bfloat16")
    SCRATCH["h" + _k] = ("sbuf", [128, TW], "bfloat16")
    SCRATCH["lq" + _k] = ("sbuf", [128, BAGS], "float8_e4m3fn_x4")
    SCRATCH["ls" + _k] = ("sbuf", [128, BAGS], "uint8")
for _o in range(2):
    for _h in range(2):
        SCRATCH["ps%d%d" % (_o, _h)] = ("psum", [128, 512], "float32")

SEMAPHORES = ["cv", "cs", "ct", "cg", "lit", "lf0", "lf1", "lob_s", "lbag_s", "lw", "lex", "inva", "invb", "invc",
              "loc", "arx", "ara", "arb", "arc", "add0", "ys"]


def rank_program(g, core, T, topo):
    rank = T.rank_of(core)
    if rank is None:
        return
    A = AluOpType
    COPY = ActivationFunctionType.Copy
    cores = list(T.cores)
    near = [r for r in range(len(cores)) if topo.host(cores[r]) == topo.host(core)]
    far = [r for r in range(len(cores)) if r not in near]
    start, at = {}, 0
    for r in range(len(cores)):
        start[r] = at
        at += NC if r in near else FC
    m0, x0 = start[near[0]], start[far[0]]
    mates = [r for r in near if topo.mates(core, cores[r])]
    who = {
        "a": [r for r in mates if topo.die(cores[r]) == topo.die(core)][0],
        "b": [r for r in mates if topo.die(cores[r]) != topo.die(core)][0],
        "c": [r for r in near if r != rank and cores[r] in topo.cores_of(core)][0],
        "d": rank,
    }

    queue = {"v": g.vector, "s": g.scalar, "t": g.tensor, "g": g, "y": g.sync}
    count = {"v": 0, "s": 0, "t": 0, "g": 0}
    seen = {}

    def done(k, ins):
        ins.then_inc(T.sem["c" + k], 1)
        count[k] += 1
        return count[k]

    def wait(q, name, n):
        if seen.get((q, name), 0) < n:
            queue[q].wait_ge(T.sem[name], n)
            seen[(q, name)] = n

    def need(q, **ks):
        for k in ks:
            wait(q, "c" + k, ks[k])

    vec, sca, ten, syn = g.vector, g.scalar, g.tensor, g.sync

    v_lob = done("v", vec.memset(T.lob[:, :], -1))
    for q in range(4):
        rows, cols = slice(32 * q, 32 * q + 32), slice(m0 + NC * q, m0 + NC * q + NC)
        syn.dma_start(T.li[rows, 0:HC], T.it[:, cols]).then_inc(T.sem.lit, 16)
        sca.dma_start(T.li[rows, HC:NC], T.it2[:, cols]).then_inc(T.sem.lit, 16)
    need("y", v=v_lob)
    need("s", v=v_lob)
    for q in range(4):
        cols = slice(m0 + NC * q, m0 + NC * q + NC)
        for h in range(2):
            queue["ys"[h]].dma_start(T.lob[32 * q:32 * q + 16, HC * h:HC * h + HC],
                                     T.ob[8 * h:8 * h + 8, cols]).then_inc(T.sem.lob_s, 16)
    for p in range(8):
        queue["ys"[p % 2]].dma_start(T.lx[16 * p:16 * p + 16, XC:2 * XC], T.it2[:, x0:x0 + XC]).then_inc(T.sem.lf1, 16)
    syn.dma_start(T.ext[:, 16:EXW], T.ex[:, :]).then_inc(T.sem.lex, 16)
    for p in range(8):
        queue["ys"[p % 2]].dma_start(T.lx[16 * p:16 * p + 16, 0:XC], T.it[:, x0:x0 + XC]).then_inc(T.sem.lf0, 16)

    g_p = done("g", g.iota(T.p1[:, :], [[0, 1]], 0, 1))
    g_kb = done("g", g.iota(T.kb[:, :], [[1, HC], [0, 2]], 0, 0))
    g_tr = done("g", g.iota(T.trash[:, :], [[16, NC]], BAGS // 4, 1))
    g_xt = done("g", g.iota(T.xtrash[:, :], [[0, 4], [16, FC]], BAGS, 1))

    v_ext = done("v", vec.memset(T.ext[:, 0:16], 0.0))
    need("v", g=g_p)
    need("g", v=done("v", vec.tensor_scalar(T.c15[:, :], T.p1[:, :], ROWS - 1, None, A.bitwise_and)))
    g.indirect_dma_start(T.lbag[:, :], None, T.bag[:], IndirectOffsetOnAxis(ap=T.c15[:, 0:1], axis=0),
                         bounds_check=ROWS - 1).then_inc(T.sem.lbag_s, 16)
    wait("g", "lit", 128)
    g.dma_start(T.wt[:, :], T.w[:, :]).then_inc(T.sem.lw, 16)
    v_win = done("v", vec.memset(T.win[:, 0:BAGS], 0))
    v3 = done("v", vec.tensor_scalar(T.c3[:, :], T.p1[:, :], 3, None, A.bitwise_and))
    need("v", g=g_kb)
    v_k = done("v", vec.tensor_copy(T.ksel[:, :], T.kb[:, :]))
    need("v", v=v3)
    v_tc = done("v", vec.tensor_scalar(T.tcol[:, :], T.c3[:, :], 12.0, None, A.add))
    done("v", vec.memset(T.acc[:, 0:ACW], 0.0))

    wait("v", "lit", 128)
    v1 = done("v", vec.tensor_scalar(T.pk1[:, :], T.li[:, HC:NC], float(PK), float(PK + 1), A.mult, A.add))
    done("v", vec.memset(T.acc[:, ACW:3 * ACW // 2], 0.0))
    need("v", v=v1)
    v_pk = done("v", vec.tensor_tensor(T.pk[:, :], T.pk1[:, :], T.li[:, 0:HC], A.add))
    need("s", v=v_pk)
    s_fb = done("s", sca.activation(T.fb[:, :], T.pk[:, :].indirect(T.ksel[:, 0:NC]), COPY))
    wait("v", "lob_s", 128)
    vl = done("v", vec.tensor_scalar(T.obl[:, :], T.lob[:, 0:NC], 3, None, A.bitwise_and))
    vh = done("v", vec.tensor_scalar(T.obh[:, :], T.lob[:, 0:NC], 4095, 2, A.bitwise_and, A.logical_shift_right))
    need("v", v=vl)
    done("v", vec.tensor_scalar(T.obq[:, :], T.obl[:, :], 64.0, None, A.mult))
    need("v", v=vh, g=g_tr)
    vm = done("v", vec.tensor_tensor(T.obm[:, :], T.obh[:, :], T.trash[:, :], A.min))
    done("v", vec.memset(T.acc[:, 3 * ACW // 2:2 * ACW], 0.0))
    need("v", v=vm)
    vs = done("v", vec.tensor_tensor(T.obs[:, :], T.obq[:, :], T.obm[:, :], A.add))
    need("v", s=s_fb)
    done("v", vec.transpose(T.ft[:, :], T.fb[:, :]))
    need("v", v=vs)
    for h in range(2):
        vo = done("v", vec.tensor_copy(T.obo[:, h:NC:2], T.obs[:, HC * h:HC * h + HC]))

    def offx(w, t):
        c = XC * (2 * t + w)
        return T.offx[:, c:c + XC]

    def far_offsets(t, a, b):
        c = 2 * XC * t
        return done("v", vec.tensor_scalar(T.offx[:, c + a:c + b], T.lx[:, a:b], 4.0, float(16 + t), A.mult, A.add))

    wait("v", "lf1", 128)
    v_ox = [far_offsets(t, XC, 2 * XC) for t in (0, 1)]
    need("v", v=vo)
    v_inv = done("v", vec.tensor_copy(T.win[:, 0:WINW].indirect(T.obo[:, 0:NC]), T.ft[:, :]))
    wait("v", "lf0", 128)
    v_ox += [far_offsets(t, 0, 2 * XC) for t in (2, 3)]
    v_ou = [far_offsets(t, 0, XC) for t in (0, 1)] + v_ox[2:]
    need("y", v=v_inv)
    def spread(eng, ts):
        for i, k in enumerate("abcd"):
            q = 32 * near.index(who[k])
            for t in ts:
                eng.dma_start(T.tab[t:128:4, 64 * i:64 * i + 64], T.win[q:q + 8, 0:BAGS]).then_inc(
                    T.sem["inv" + min(k, "c")], 16)

    spread(syn, range(4))

    wait("s", "lex", 16)
    s_vx = {}
    for t in range(4):
        need("s", v=max(v_ext, v_ox[t]))
        s_vx[t] = done("s", sca.activation(T.vx[:, t:4 * NX:4], T.ext[:, :].indirect(offx(1, t)), COPY))
    wait("v", "lex", 16)
    for t in range(4):
        need("v", s=s_vx[t], v=v_ou[t])
        vh = done("v", vec.tensor_tensor(T.hx[:, t:4 * NX:4], T.ext[:, :].indirect(offx(0, t)),
                                         T.vx[:, t:4 * NX:4], A.add))
    def second(a, b):
        return done("v", vec.tensor_scalar(T.ofv[:, a:b], T.tab[:, a:b], 4.0 / PK, T.tcol[:, 0:1], A.mult, A.add))

    def lower(a, b):
        return done("v", vec.tensor_scalar(T.low[:, a:b], T.tab[:, a:b], PK - 1, None, A.bitwise_and))

    def first(a, b, n=None):
        if n:
            need("v", v=n)
        return done("v", vec.tensor_scalar(T.ofu[:, a:b], T.low[:, a:b], 4.0, T.tcol[:, 0:1], A.mult, A.add))

    wait("v", "inva", 64)
    v_of = {("a", "v"): second(0, 64)}
    wait("v", "lbag_s", 16)
    v_bz = done("v", vec.tensor_scalar(T.bgz[:, :], T.lbag[:, x0:x0 + XC], 1023, None, A.bitwise_and))
    need("v", v=vh)
    need("g", v=done("v", vec.quantize_mx(T.qx[:, :], T.sx[:, :], T.hx[:, :])))

    me = near.index(rank)
    off_chip = topo.engines(core, cores[who["a"]])
    n_x = len(off_chip) // 4
    local = [8 * n_x]
    for src, dst in ((T.qx, T.lqx), (T.sx, T.lsx)):
        tr = []
        for k in range(4):
            d = cores[far[k]]
            es = topo.engines(core, d)[n_x * k:n_x * (k + 1)]
            rid, pid = topo.addr(d, core)
            a, b = src[:, FAR * k:FAR * k + FAR], dst[:, FAR * me:FAR * me + FAR]
            if src is T.qx:
                a, b = a.bitcast(dt.uint8), b.bitcast(dt.uint8)
            tr.append(RemoteDMATransfer(dst_ids=[DstId(rid=rid, pnc=pid)], src=a, dst=b, remote_sem=T.sem.arx,
                                        dma_engine_mask=sum(1 << e for e in es)))
        g.remote_dma_fused(tr, local_sem=T.sem.loc)

    def offs(k, u, a, b):
        c = 64 * "abcd".index(k)
        return T["of" + u][:, c + a // 4:c + b // 4]

    def pick(k, u, a, b, out):
        need("s", v=v_of[k, u])
        return done("s", sca.activation(out, T.ext[:, :].indirect(offs(k, u, a, b)), COPY))

    def join(k, a, b, s, second, out):
        need("v", s=s, v=v_of[k, "u"])
        return done("v", vec.tensor_tensor(out, T.ext[:, :].indirect(offs(k, "u", a, b)), second, A.add))

    def quant(k, a, b, tile):
        return done("v", vec.quantize_mx(T["q" + k][:, a:b], T["s" + k][:, a:b], tile))

    def send(k, n, es):
        need("g", v=n)
        d = cores[who[k]]
        rid, pid = topo.addr(d, core)
        m = sum(1 << e for e in es)
        g.remote_dma(T["lq" + k][:, :].bitcast(dt.uint8), T["q" + k][:, :].bitcast(dt.uint8),
                     T.sem["ar" + k], T.sem.loc, pid, rid, m)
        g.remote_dma(T["ls" + k][:, :], T["s" + k][:, :], T.sem["ar" + k], T.sem.loc, pid, rid, m)
        local[0] += 2 * len(es)

    low_a = lower(0, 64)
    need("v", v=v_bz, g=g_xt)
    v_bm = done("v", vec.tensor_tensor(T.bgm[:, :], T.bgz[:, :], T.xtrash[:, :], A.min))
    wait("v", "invb", 64)
    v_of["b", "v"] = second(64, 128)
    low_b = lower(64, 128)
    v_of["a", "u"] = first(0, 64, low_a)
    need("v", v=v_bm)
    for o in range(2):
        v_bl = done("v", vec.tensor_scalar(T.bl[:, :, FC * o:FC * o + FC], T.bgm[:, :], float(ACW * o), None, A.add))
    c1, c2 = CUTS
    sa = [pick("a", "v", a, b, T.va[:, 4 * a:4 * b]) for a, b in ((0, c1), (c1, c2))]
    vp = done("v", vec.tensor_copy(T.va[:, 4 * c2:TW], T.ext[:, :].indirect(offs("a", "v", c2, BAGS))))
    join("a", 0, c1, sa[0], T.va[:, 0:4 * c1], T.ha[:, 0:4 * c1])
    v_of["b", "u"] = first(64, 128, low_b)
    need("v", v=vp)
    join("a", c2, BAGS, sa[0], T.va[:, 4 * c2:TW], T.ha[:, 4 * c2:TW])
    n = join("a", c1, c2, sa[1], T.va[:, 4 * c1:4 * c2], T.ha[:, 4 * c1:4 * c2])
    wait("v", "invc", 128)
    v_of["c", "v"] = v_of["d", "v"] = second(128, 256)
    v_low = lower(128, 256)
    need("v", v=n)
    n = quant("a", 0, 256, T.ha[:, :])
    send("a", n, off_chip)
    v_of["c", "u"] = v_of["d", "u"] = first(128, 256, v_low)
    sb = pick("b", "v", 0, 256, T.vb[:, :])
    n = join("b", 0, 256, sb, T.vb[:, :], T.hb[:, :])
    wait("v", "lw", 16)
    v_qw = done("v", vec.quantize_mx(T.wq[:, :], T.ws[:, :], T.wt[:, :]))
    need("v", v=n)
    n = quant("b", 0, 256, T.hb[:, :])
    send("b", n, off_chip)
    sc = pick("c", "v", 0, 256, T.vc[:, :])
    n = join("c", 0, 256, sc, T.vc[:, :], T.hc[:, :])

    def upper(a, b):
        return slice(4 * (a - HB), 4 * (b - HB))

    def piece(i):
        a, b = HB + PIECE * i, HB + PIECE * (i + 1)
        return join("d", a, b, sd[min(i, 1)], T.vd1[:, upper(a, b)], T.hd1[:, upper(a, b)])

    pick("d", "u", 0, HB, T.hd0[:, :])
    need("g", s=pick("d", "v", 0, HB, T.vd0[:, :]))
    g.dma_start(T.hd0[:, :], T.vd0[:, :], accum_op=A.add).then_inc(T.sem.add0, 16)
    sd = [pick("d", "v", HB, HB + PIECE, T.vd1[:, upper(HB, HB + PIECE)])]
    piece(0)
    need("v", v=n)
    n_c = quant("c", 0, 256, T.hc[:, :])
    send("c", n_c, [e for e in topo.engines(core, cores[who["c"]]) if e in off_chip])

    def mm(out, o, q, s, first, last):
        return done("t", ten.matmul_mx(out, T.wq[:, 128 * o:128 * o + 128], T.ws[:, 128 * o:128 * o + 128],
                                       q, s, first, last))

    need("t", v=v_qw)
    wait("t", "arx", 8 * n_x)
    for o in range(2):
        n = mm(T["px%d" % o][:, 0:NX], o, T.lqx[:, :], T.lsx[:, :], True, True)
        need("s", t=n)
        s_x = done("s", sca.activation(T.xs[:, :, FAR * o:FAR * o + FAR], T["px%d" % o][:, 0:NX], COPY))
    sd.append(pick("d", "v", HB + PIECE, BAGS, T.vd1[:, upper(HB + PIECE, BAGS)]))

    v_d = {}

    def quant_upper():
        v_d[1] = quant("d", HB, BAGS, T.hd1[:, :])

    def quant_lower():
        wait("v", "add0", 16)
        v_d[0] = quant("d", 0, HB, T.hd0[:, :])

    fill = [lambda: piece(1), lambda: piece(2), lambda: piece(3), None, quant_upper, quant_lower, None]
    need("v", s=s_x, v=v_bl)
    for step in range(7):
        k = (step + 1) // 2
        acc = T.acc[:, :].indirect(T.bl[:, k, :])
        if step % 2:
            n = done("v", vec.tensor_tensor(T.tm[:, k, :], acc, T.xs[:, k, :], A.add))
        else:
            n = done("v", vec.tensor_copy(acc, (T.tm if k else T.xs)[:, k, :]))
        if fill[step]:
            fill[step]()
        need("v", v=n)
    v_far = n

    last = {}
    order = ["a0", "a1", "b0", "b1", "d1", "c1", "c0", "d0"]
    for k, h in [(x[0], int(x[1])) for x in order]:
        if k == "d":
            need("t", v=v_d[h])
            q, s = T.qd, T.sd
        else:
            wait("t", "ar" + k, 2 * len(off_chip))
            q, s = T["lq" + k], T["ls" + k]
        cols = slice(HB * h, HB * h + HB)
        last[h] = [mm(T["ps%d%d" % (o, h)][:, 0:HB], o, q[:, cols], s[:, cols], k == "a", k == "dc"[h])
                   for o in range(2)]
    for h in (1, 0):
        for o in range(2):
            need("v", t=last[h][o], v=v_far)
            c = BAGS * o + HB * h
            n = done("v", vec.tensor_tensor(T.yb[:, c:c + HB], T["ps%d%d" % (o, h)][:, 0:HB],
                                            T.acc[:, ACW * o + HB * h:ACW * o + HB * h + HB], A.add))
            q = "ys"[o]
            need(q, v=n)
            queue[q].dma_start(T.y[:, c:c + HB], T.yb[:, c:c + HB]).then_inc(T.sem.ys, 16)
    wait("g", "loc", local[0])
    wait("y", "ys", 64)
    need("y", s=count["s"], t=count["t"], g=count["g"])
